import numpy as np, ml_dtypes
CORES = [1,5,17,21,33,37,49,53]
N = 8
BF = ml_dtypes.bfloat16
D, L, H, S1, S2, VI = 3712, 128, 64, 3, 5, 4
def effects(rng):
    cap = rng.integers(1, 256, (N, 8, 1, D))
    return np.minimum((rng.random((N, 8, 16, D)) * (cap + 1)).astype(np.int64), cap)
def near(rng, n, share, few=64):
    pop = rng.integers(0, D, (N, 8, few)); v = rng.integers(0, D, (N, 8, 16, n))
    c = np.take_along_axis(pop, rng.integers(0, few, (N, 8, 16 * n)), 2).reshape(N, 8, 16, n)
    return np.where(rng.random(v.shape) < share, c, v)
def rows(rng, n):
    return np.argsort(np.argsort(rng.random((N, 8, 16, L)), axis=2), axis=2) < n
def forest(rng, filled, own, deep):
    o = np.argsort(np.where(filled, rng.random(filled.shape), 2.0), axis=2); r = np.arange(16)[:, None]
    u = rng.random(filled.shape); b = np.minimum((rng.random(filled.shape) * (r + 1)).astype(np.int64), r)
    b = np.where(u < own, r, np.where(u > 1 - deep, np.maximum(r - 1, 0), b))
    w = np.zeros(filled.shape, np.int64); np.put_along_axis(w, o, np.take_along_axis(o, b, 2), 2)
    return np.where(filled, w, 0)
def pack(eff, rem, lim, drugs, why, filled):
    return {"eff": np.ascontiguousarray(eff.reshape(N, 128, D)).astype(np.float32).astype(BF), "rem": np.ascontiguousarray(rem.reshape(N, 128, D)).astype(np.int32),
            "lim": np.repeat(lim, 16, axis=1)[:, :, None].astype(np.int32), "drugs": np.ascontiguousarray(np.where(filled, drugs, D).reshape(N, 128, L)).astype(np.int32),
            "why": np.ascontiguousarray(np.where(filled, why, 0).reshape(N, 128, L)).astype(np.int32)}
def setup_inputs(rng):
    n = np.maximum(rng.integers(0, 17, (N, 8, 1, L)), rng.integers(0, 17, (N, 8, 1, L)))
    filled = rows(rng, n); why = forest(rng, filled, 0.3, 0.3)
    return pack(effects(rng), near(rng, D, 0.3), rng.integers(6000, 20000, (N, 8)), near(rng, L, 0.3), why, filled)
def setup_inputs_ties(rng):
    v = rng.integers(0, 256, (N, 8, 16)); v[:, :, 0] = 255
    sh = rng.integers(0, 16, (N, 8, 1, D)); sh[:, ::2, :, 1::2] = sh[:, ::2, :, ::2] + 8
    ix = (np.arange(16)[:, None] + sh) % 16
    eff = np.take_along_axis(v, ix.reshape(N, 8, 16 * D), 2).reshape(N, 8, 16, D)
    lim = np.minimum(rng.integers(3, 12, (N, 8)) * np.add.reduce(v, axis=2), 65280)
    filled = rows(rng, rng.integers(1, 17, (N, 8, 1, L))); drugs = near(rng, L, 0.9, 6)
    pair = rng.random((N, 8, 1, L)) < 0.5; pair[:, 1::2] = False
    twin = np.repeat(drugs[:, :, ::2], 2, axis=2); twin[:, :, 1::2] = twin[:, :, 1::2] ^ 1
    drugs = np.where(pair, twin, drugs); filled = np.where(pair, np.repeat(filled[:, :, ::2], 2, axis=2), filled)
    why = forest(rng, filled, 0.4, 0.2)
    return pack(eff, near(rng, D, 0.7, 6), lim, drugs, why, filled)
def setup_inputs_corners(rng):
    eff = effects(rng); eff[..., 0] = 0; eff[..., D - 1] = 255
    lim = rng.choice(np.array([1, 12000, 65280]), (N, 8)); lim[:, 1] = 1; lim[:, 2] = 65280
    kind = rng.integers(0, 10, (N, 8, 1, L)); m = np.arange(16)[:, None]; hv = rng.random((N, 8, 1, L)) < 0.5
    filled = rows(rng, np.where(kind == 6, 15, rng.integers(0, 17, (N, 8, 1, L))))
    filled = filled | (kind == 1) | (kind == 2) | (kind == 5) | (kind == 8) | (kind == 9)
    filled = np.where(kind == 0, False, np.where(kind == 3, m == 15, np.where(kind == 4, m == 0, filled)))
    why = forest(rng, filled, 0.2, 0.2)
    for k, w in ((1, np.maximum(m - 1, 0)), (2, m), (5, 0 * m), (8, np.minimum(m + 1, 15)), (9, 0 * m + 15)):
        why = np.where(kind == k, w, why)
    drugs = near(rng, L, 0.3)
    low = (kind == 1) | (kind == 5); high = (kind == 8) | (kind == 9)
    top = (low & (m == np.where(hv, 0, 15))) | (high & (m == np.where(hv, 15, 0)))
    drugs = np.where(top | (kind == 3), D - 1, np.where(kind == 4, 0, drugs))
    return pack(eff, near(rng, D, 0.3), lim, drugs, why, filled)
def setup_inputs_great(rng):
    low = np.array([11, 0, 1, 0, 11, 0, 0, 11]).reshape(8, 1, 1); lane = np.arange(L)
    eff = effects(rng); rem = near(rng, D, 0.3); drugs = near(rng, L, 0.3); lim = rng.integers(6000, 20000, (N, 8))
    filled = rows(rng, rng.integers(low, 16, (N, 8, 1, L)))
    for g in (1, 6):
        eff[:, g] = rng.integers(0, 16, (N, 16, D)) < np.array([0, 1, 2, 4, 6, 8, 12, 16])[np.arange(D) % 8]
        lim[:, g] = 1
        h = np.maximum(rng.integers(-4, 8, (N, 1, L)), 0); pure = rng.random((N, 1, L)) < 0.6
        drugs[:, g] = np.where(pure, drugs[:, g] // 8 * 8 + h, drugs[:, g])
        filled[:, g] = filled[:, g] | (pure & (h == 0))
        faint = rng.random((N, 1, D)) < 0.3
        rem[:, g] = np.where(faint, rem[:, g] // 8 * 8 + rng.integers(0, 2, (N, 16, D)), rem[:, g])
    eff[:, 2] = rng.integers(0, 101, (N, 16, D)); lim[:, 2] = 1
    for q in range(N):
        o = rng.permutation(D); i = rng.integers(0, 16, L)
        eff[q, 2][:, o[:L]] = rng.integers(128, 256, (16, L))
        v = rng.choice(o[L:], (16, L)); v[i, lane] = o[:L]; drugs[q, 2] = v
        filled[q, 2][i, lane] = True
    for g in (0, 4, 7):
        eff[:, g] = rng.integers(0, 32, (N, 16, D)) + rng.integers(192, 225, (N, 1, 1))
        if g == 7:
            eff[:, g, :, 7::8] = 255
            drugs[:, g, :, L - 1] = drugs[:, g, :, L - 1] // 8 * 8 + 7
            filled[:, g, :, L - 1] = np.arange(16)[None, :] != rng.integers(0, 16, (N, 1))
        e = np.add.reduce(eff[:, g], axis=1)
        b = np.add.reduce(np.where(filled[:, g], np.take_along_axis(e, drugs[:, g].reshape(N, 16 * L), 1).reshape(N, 16, L), 0), axis=1)
        i = np.argmax(rng.random((N, L)) * (b % 128 > 0), axis=1); v = b[np.arange(N), i]
        lim[:, g] = v + (v % 256 > 128)
    lim[N - 1, 7] = 61200
    filled[0] = True; filled[2] = True
    o = rng.permutation(8 * L)[:int(rng.integers(100, 201))]
    for j in o: filled[2, j // L, :, j % L] = False
    return pack(eff, rem, lim, drugs, forest(rng, filled, 0.3, 0.3), filled)
def setup_inputs_spread(rng):
    cap = np.exp2(8 * rng.random((N, 8, 1, D))).astype(np.int64); cap = np.minimum(cap, 255)
    eff = np.minimum((rng.random((N, 8, 16, D)) * (cap + 1)).astype(np.int64), cap)
    e = rng.choice(np.array([1.0, 3.0, 8.0]), (N, 8, 1, 1))
    rem = np.minimum((D * rng.random((N, 8, 16, D)) ** 3).astype(np.int64), D - 1); drugs = np.minimum((D * rng.random((N, 8, 16, L)) ** e).astype(np.int64), D - 1)
    lim = np.minimum(np.maximum(np.exp2(16 * rng.random((N, 8))).astype(np.int64), 1), 65280); lim[:, 5] = rng.integers(3000, 9000, N)
    filled = rows(rng, rng.integers(0, 17, (N, 8, 1, L))); why = forest(rng, filled, rng.random((N, 8, 1, L)), 0.3)
    return pack(eff, rem, lim, drugs, why, filled)
def setup_inputs_ends(rng):
    eff = 255 * (rng.random((N, 8, 16, D)) < rng.choice(np.array([0.0, 0.5, 1.0]), (N, 8, 1, D))).astype(np.int64)
    case = rng.integers(0, 4, (N, 8)); case[0, 0] = 1; case[N - 1, 7] = 0; case[:, 4] = 2
    a = np.where((case == 0) | (case == 3), 255, np.where(case == 1, 0, -1))[:, :, None]; b = np.where(case == 0, 255, np.where((case == 1) | (case == 3), 0, -1))[:, :, None]
    eff[..., 0] = np.where(a >= 0, a, eff[..., 0]); eff[..., D - 1] = np.where(b >= 0, b, eff[..., D - 1])
    rem = (D - 1) * rng.integers(0, 2, (N, 8, 16, D))
    lim = np.where(rng.random((N, 8)) < 0.5, 1, 65280); lim[:, 0] = 1; lim[:, 7] = 65280
    filled = rng.random((N, 8, 16, L)) < 0.65; filled[:, :, 0] = True; filled[:, :, 15] = True
    none = rng.random((N, 8, 1, L)) < 0.05; full = rng.random((N, 8, 1, L)) < 0.1; full[..., 1] = True; full[..., L - 1] = True
    filled = full | (filled & ~none)
    drugs = np.where(rng.random((N, 8, 16, L)) < 0.7, 0, D - 1); drugs[..., 1] = 0; drugs[..., L - 1] = D - 1
    why = 15 * rng.integers(0, 2, (N, 8, 16, L)); z = rng.integers(0, 2, (N, 8, L))
    why[:, :, 0] = 15 * z; why[:, :, 15] = np.where(z == 1, 15, why[:, :, 15])
    return pack(eff, rem, lim, drugs, why, filled)
def check_inputs(d):
    bad = []
    for k, lo, hi in (("eff", 0, 255), ("rem", 0, D - 1), ("lim", 1, 65280), ("drugs", 0, D), ("why", 0, 15)):
        v = np.asarray(d[k]).astype(np.float64)
        if not (np.min(v) >= lo and np.max(v) <= hi): bad.append("range of " + k)
        elif k == "eff" and np.any(v != np.floor(v)): bad.append("whole numbers in eff")
    v = np.asarray(d["lim"]).reshape(N, 8, 16)
    if np.any(v != v[:, :, :1]): bad.append("lim alike in a group")
    if "range of drugs" in bad or "range of why" in bad: return bad
    filled = np.asarray(d["drugs"]).reshape(N, 8, 16, L) < D; w = np.asarray(d["why"]).astype(np.int64).reshape(N, 8, 16, L)
    if np.any(~filled & (w != 0)): bad.append("why is 0 in empty rows")
    if np.any(filled & ~np.take_along_axis(filled, w, 2)): bad.append("reasons are filled rows")
    c = w
    for _ in range(4): c = np.take_along_axis(c, c, 2)
    if np.any(filled & (np.take_along_axis(w, c, 2) != c)): bad.append("reasons end in a row that is its own reason")
    return bad
def stand(A, a, t):
    return np.concatenate([A[(a - S1 * t) % N][..., :H], A[(a - S2 * t) % N][..., H:]], axis=2)
def reference(eff, rem, lim, drugs, why):
    X = eff.astype(np.float32).astype(np.int32).reshape(N, 8, 16, D)
    X = np.concatenate([X, np.zeros((N, 8, 16, 1), np.int32)], axis=3)
    R = rem.astype(np.int64).reshape(N, 8, 16, D); B = lim.astype(np.int64).reshape(N, 8, 16)[:, :, :1]
    P = drugs.astype(np.int64).reshape(N, 8, 16, L); Q = why.astype(np.int64).reshape(N, 8, 16, L)
    m16 = np.arange(16)[None, :, None]; c = np.zeros(N, np.int64)
    for t in range(VI):
        NP = np.zeros_like(P); NQ = np.zeros_like(Q); stops = np.zeros(N, np.int64)
        for a in range(N):
            p = stand(P, a, t); w = stand(Q, a, t); filled = p < D
            x = np.take_along_axis(X[a], p.reshape(8, 1, 16 * L), 2).reshape(8, 16, 16, L)
            T = np.add.reduce(x, axis=2); burden = np.add.reduce(T, axis=1)
            stop = np.any(filled, axis=1) & ((burden >= B[a] + c[a]) | np.all(filled, axis=1))
            s = np.argmax(np.where(filled, np.add.reduce(x, axis=1), -1), axis=1)[:, None, :]
            cur = np.broadcast_to(m16, p.shape); reach = np.zeros(p.shape, bool)
            for _ in range(16):
                reach = reach | (cur == s); cur = np.take_along_axis(w, cur, 1)
            gone = reach & filled & stop[:, None, :]
            d = np.take_along_axis(p, s, 1)[:, 0]; xs = np.take_along_axis(x, s[:, None], 2)[:, :, 0]; xn = (xs + (T >> 4)) >> 1
            p = np.where(gone, D, p); w = np.where(gone, 0, w); filled = p < D; some = np.any(filled, axis=1)
            U = np.add.reduce(np.where(filled[:, None], x, 0), axis=2)
            f = np.argmax(U, axis=1)
            k = np.argmax(np.where(filled, np.take_along_axis(x, f[:, None, None, :], 1)[:, 0], -1), axis=1)
            dk = np.minimum(np.take_along_axis(p, k[:, None, :], 1), D - 1)
            cand = np.take_along_axis(R[a], dk, 2)
            xc = np.take_along_axis(X[a], cand.reshape(8, 1, 16 * L), 2).reshape(8, 16, 16, L)
            score = np.add.reduce(np.abs(255 - xc - (U >> 4)[:, :, None, :]), axis=1)
            new = np.take_along_axis(cand, np.argmin(score, axis=1)[:, None, :], 1)
            put = (m16 == np.argmin(filled, axis=1)[:, None, :]) & some[:, None, :]
            p = np.where(put, new, p); w = np.where(put, k[:, None, :], w)
            for A, v in ((NP, p), (NQ, w)):
                A[(a - S1 * t) % N, :, :, :H] = v[..., :H]; A[(a - S2 * t) % N, :, :, H:] = v[..., H:]
            for g in range(8):
                lanes = np.flatnonzero(stop[g]); u, i = np.unique(d[g, lanes], return_index=True)
                X[a, g][:, u] = xn[g][:, lanes[i]]
            stops[a] = np.count_nonzero(stop)
        P, Q, c = NP, NQ, stops & 255
    yp = np.stack([stand(P, a, VI - 1) for a in range(N)]); yq = np.stack([stand(Q, a, VI - 1) for a in range(N)])
    return {"yp": yp.reshape(N, 128, L).astype(np.float32), "yq": yq.reshape(N, 128, L).astype(np.float32),
            "yx": np.ascontiguousarray(X[..., :D]).reshape(N, 128, D).astype(np.float32).astype(BF)}

@@ -1,0 +1,494 @@
+from concourse.bass import DstId, RemoteDMATransfer
+from concourse.mybir import dt, AluOpType, AxisListType, ActivationFunctionType
+import comms_topo
+
+D, VI, S1, S2, NR = 3712, 4, 3, 5, 8
+XW = 3856
+BIGM = 12582912.0
+VS2, VS1 = 36, 32
+
+SCRATCH = {}
+PLACE = {}
+_used = {}
+
+
+def _own(dtype, cols, names):
+    for n in names.split():
+        SCRATCH[n] = ("sbuf", [128, cols], dtype); PLACE[n] = (n, 0, cols)
+
+
+def _small(dtype, cols, names):
+    for n in names.split():
+        a = _used.get(dtype, 0)
+        PLACE[n] = ("pool_" + dtype, a, cols); _used[dtype] = a + (cols + 15) // 16 * 16
+        SCRATCH["pool_" + dtype] = ("sbuf", [128, _used[dtype]], dtype)
+
+
+_own("bfloat16", XW, "X X2"); _own("int32", D, "RM")
+CH = (("v", 0, 32), ("s", 32, 24), ("v", 56, 32), ("v", 88, 24), ("v", 112, 16))
+CB = ("B3", "B6", "B3", "B6", "B4")
+_own("bfloat16", 2048, "x1 x2 xpd dif adf sg0"); _own("float16", 2048, "sig")
+for _k in range(VI):
+    _own("uint16", 128, "LD%d" % _k); _own("float32", 128, "LA%d" % _k); _own("bfloat16", 128, "LW%d" % _k)
+    if _k: _own("uint16", 128, "SD%d" % _k); _own("float32", 128, "SA%d" % _k); _own("bfloat16", 128, "SW%d" % _k)
+_own("int32", 128, "drg whyi"); _own("float32", 128, "yps yqs"); _own("int32", 8, "limi")
+_small("int32", 128, "d0i mqi zi gi xni xnh bcoi"); _small("int32", 16, "mi p63 kki kk4 cnti cntj si0 si1 si2 si3")
+_small("uint16", 128, "bco offp cand"); _small("uint16", 16, "bco31 selo dkl dls")
+_small("bfloat16", 128, "one zt1 zt2 bo bo16 nbo bom id1 idn id64 idg idm idu idn16 idn64 wput mq dkc c15b c15x16 pow2 emp r1 r2 "
+       "ohs gs st sg1 emq rq ohk ohkb tf wa wc e0")
+_small("bfloat16", 256, "c15r rs32 rs16 rs2 cj1 cj2 put2 putb zz oh"); _small("bfloat16", 1024, "onesel sela sel ebuf")
+_small("bfloat16", 16, "bc2 stc wt"); _small("float16", 128, "d16 d16p yd r16 hi16 c16 yds")
+_small("float32", 128, "d0 t0 id32 idn32 id256 bo32 one32 powf pwr half zero acs usb ur tsb tr skm dks ya zl fil v0 vt vm wc1 neq c15f nrs mf")
+_small("float32", 256, "key1 hor scm aw1"); _small("float32", 16, "limf lims8 sgn cb cnt cjunk dsc fst fs u1 u2 u3 wcol thr pcol smv")
+for _k in range(8): SCRATCH["B%d" % _k] = ("psum", [128, 512], "float32")
+
+SEMAPHORES = ["qv", "qs", "qp", "qg"] + ["arr%s%d" % (a, t) for a in "DAW" for t in range(1, VI)] \
+    + ["loc%s%d" % (a, t) for a in "DAW" for t in range(1, VI)] + ["dm%d" % i for i in range(11)]
+
+
+def rank_program(g, core, T, topo):
+    rank = T.rank_of(core)
+    if rank is None:
+        return
+    A = AluOpType; F = ActivationFunctionType
+    V, S, P = g.vector, g.scalar, g.tensor
+    q_of = {"v": V, "s": S, "p": P, "g": g, "y": g.sync}
+    cnt = {"v": 0, "s": 0, "p": 0, "g": 0}
+    known = {q: {} for q in q_of}
+    writer = {}; readers = {}; snap = {}; total = {}
+
+    def b(name, lo=0, hi=None, step=None):
+        n, o, w = PLACE[name]
+        hi = w if hi is None else hi
+        return T[n][:, o + lo:o + hi] if step is None else T[n][:, o + lo:o + hi:step]
+
+    def row(name, lo=0, hi=None):
+        n, o, w = PLACE[name]
+        return T[n][0:1, o + lo:o + (w if hi is None else hi)]
+
+    def need(q, R, W):
+        deps = []
+        for k in R:
+            if k in writer: deps.append(writer[k])
+            if k[0] == "B": deps += [r for r in readers.get(k, []) if r[2] != q]
+        for k in W:
+            if k in writer: deps.append(writer[k])
+            deps += readers.get(k, [])
+        for sem, val, dq in deps:
+            if q == "p" and dq == "p": continue
+            if known[q].get(sem, 0) >= val: continue
+            q_of[q].wait_ge(T.sem[sem], val)
+            known[q][sem] = val
+            for s2, v2 in snap.get((sem, val), {}).items():
+                if known[q].get(s2, 0) < v2: known[q][s2] = v2
+
+    def done(q, R, W, sem, val, who):
+        snap[(sem, val)] = dict(known[q]); total[sem] = val
+        for k in R: readers.setdefault(k, []).append((sem, val, who))
+        for k in W:
+            writer[k] = (sem, val, who); readers[k] = []
+
+    def op(q, f, R, W):
+        R = R.split(); W = W.split()
+        need(q, R, W)
+        cnt[q] += 1
+        f().then_inc(T.sem["q" + q], 1)
+        done(q, R, W, "q" + q, cnt[q], q)
+
+    ndma = [0]
+
+    def dma(q, out, in_, R, W):
+        R = R.split(); W = W.split()
+        need(q, R, W)
+        sem = "dm%d" % ndma[0]; ndma[0] += 1
+        q_of[q].dma_start(out, in_).then_inc(T.sem[sem], 16)
+        done(q, R, W, sem, 16, "dma")
+
+    def ts(out, in0, s1, s2, o0, o1, R, W):
+        if o1 is None: op("v", lambda: V.tensor_scalar(out, in0, s1, None, o0), R, W)
+        else: op("v", lambda: V.tensor_scalar(out, in0, s1, s2, o0, o1), R, W)
+
+    def tt(out, in0, in1, o, R, W): op("v", lambda: V.tensor_tensor(out, in0, in1, o), R, W)
+
+    def tc(out, in_, R, W): op("v", lambda: V.tensor_copy(out, in_), R, W)
+
+    def scan(out, d0, d1, init, o0, o1, R, W): op("v", lambda: V.tensor_tensor_scan(out, d0, d1, init, o0, o1), R, W)
+
+    def act(out, in_, fn, R, W, bias=0.0, scale=1.0, acc=None):
+        if acc is None: op("s", lambda: S.activation(out, in_, fn, bias=bias, scale=scale), R, W)
+        else: op("s", lambda: S.activation(out, in_, fn, bias=bias, scale=scale, accum_out=acc), R, W)
+
+    def mm(out, l, r, start, stop, R, W): op("p", lambda: P.matmul(out, l, r, start, stop), R, W)
+
+    def fill(name, c): op("v", lambda: V.memset(b(name), c), "", name)
+
+    def iota(name, pattern, base, cm):
+        if "int32" in PLACE[name][0]: op("g", lambda: g.iota(b(name), pattern, base, cm), "", name)
+        else: op("g", lambda: g.iota(b(name), pattern, base, cm, allow_small_or_imprecise_dtypes=True), "", name)
+
+    def sel(out, in_, pattern, base, cm): op("g", lambda: g.affine_select(b(out), b(in_), pattern, A.is_ge, 0.0, base, cm), in_, out)
+
+    dma("s", b("whyi"), T.why[:, :], "", "whyi")
+    dma("y", b("drg"), T.drugs[:, :], "", "drg")
+    dma("s", T.X[:, 0:1856], T.eff[:, 0:1856], "", "Xl0")
+    dma("y", T.X[:, 1856:D], T.eff[:, 1856:D], "", "Xl1")
+    dma("y", T.limi[:, 0:1], T.lim[:, :], "", "limi")
+    dma("y", T.RM[:, :], T.rem[:, :], "", "RM")
+
+    op("v", lambda: V.memset(T.X[:, D:XW], -1.0), "", "Xl2")
+    fill("one", 1.0); fill("half", 0.5); fill("zero", 0.0); fill("cb", 0.5)
+    scan(b("pwr"), b("half"), b("zero"), 2.0 ** 64, A.mult, A.add, "half zero", "pwr")
+    iota("rs16", [[0, 16], [1, 16]], 0, 0)
+    iota("d0", [[-1, 128]], 0, 1)
+    iota("bcoi", [[1, 128]], 0, 0)
+    iota("mf", [[0, 8], [1, 16]], 0, 0)
+    ts(b("rs16"), b("rs16"), 0.0, None, A.is_gt, None, "rs16", "rs16")
+    ts(b("rs2"), b("rs16"), 2.0, None, A.mult, None, "rs16", "rs2")
+    ts(b("nrs"), b("rs16", 0, 128), -1.0, 1.0, A.mult, A.add, "rs16", "nrs")
+    scan(b("powf"), b("rs2", 0, 128), b("nrs"), 0.0, A.mult, A.add, "rs2 nrs", "powf")
+    ts(b("id1"), b("d0"), 0.0, None, A.is_equal, None, "d0", "id1")
+    tc(b("bco"), b("bcoi"), "bcoi", "bco")
+    tt(b("t0"), b("pwr"), b("id1"), A.mult, "pwr id1", "t0")
+    op("v", lambda: V.tensor_reduce(b("wcol", 0, 1), b("t0"), AxisListType.X, A.add), "t0", "wcol")
+    ts(b("thr", 0, 1), b("wcol", 0, 1), 2.5, None, A.mult, None, "wcol", "thr")
+    tc(b("LW0"), b("whyi"), "whyi", "LW0")
+    mm(T.B5[:, 384:512], b("LW0"), b("id1"), True, True, "LW0 id1", "B5")
+    tt(b("neq"), T.B5[:, 384:512], b("mf"), A.not_equal, "B5 mf", "neq")
+    ts(b("wc1"), T.B5[:, 384:512], 1.0, 65536.0, A.add, A.mult, "B5", "wc1")
+    tt(b("vt"), b("wc1"), b("neq"), A.mult, "wc1 neq", "vt")
+    tt(T.B6[:, 0:128], b("vt"), b("powf"), A.add, "vt powf", "B6")
+
+    def closure(lo, hi):
+        for c in range(hi, lo - 1, -1):
+            K = 65536.0 * (c + 1)
+            ts(b("smv", 0, 8), T.B6[:, c:128:16], -K, None, A.add, None, "B6", "smv")
+            ts(b("vm"), T.B6[:, 0:128], K, None, A.is_ge, None, "B6", "vm")
+            tt(b("vt"), b("smv").indirect(b("bco", 0, 8)), b("vm"), A.mult, "smv bco vm", "vt")
+            if c: tt(T.B6[:, 0:128], T.B6[:, 0:128], b("vt"), A.add, "B6 vt", "B6")
+            else: tt(b("v0"), T.B6[:, 0:128], b("vt"), A.add, "B6 vt", "v0")
+
+    sel("zt1", "one", [[-16, 8], [0, 16]], 0, 1)
+    sel("bo", "zt1", [[16, 8], [0, 16]], 15, -1)
+    iota("c15r", [[0, 16], [-1, 16]], 15, 0)
+    iota("rs32", [[0, 8], [1, 32]], 0, 0)
+    iota("si0", [[0, 16]], 0, 1)
+    iota("si1", [[32, 16]], 16, 0)
+    iota("d0i", [[-1, 128]], 0, 1)
+    iota("c15f", [[0, 8], [-1, 16]], 15, 0)
+    op("g", lambda: g.affine_select(b("zt2"), b("bo"), [[1, 128]], A.is_ge, 0.0, -1, -1), "bo", "zt2")
+    iota("e0", [[-16, 8], [0, 16]], 0, 1)
+    sel("zt1", "e0", [[-16, 8], [0, 16]], 0, 1)
+    sel("bom", "zt1", [[16, 8], [0, 16]], 15, -1)
+    iota("cj2", [[0, 16], [-64, 16]], 0, 0)
+    iota("cj1", [[0, 256]], 4325376, 0)
+    iota("pcol", [[0, 16]], 1864, 1)
+    op("g", lambda: g.iota(b("onesel"), [[0, 1024]], 1, 0, allow_small_or_imprecise_dtypes=True), "", "onesel")
+    sel("sela", "onesel", [[-16, 8], [0, 128]], 0, 1)
+    sel("sel", "sela", [[16, 8], [0, 128]], 15, -1)
+    for h in range(2):
+        o = T.xpd[:, 1024 * h:1024 * h + 1024]
+        op("g", lambda: g.affine_select(b("sela"), b("onesel"), [[1, 1024]], A.is_ge, 0.0, 1024 * h, -16), "onesel", "sela")
+        op("g", lambda: g.affine_select(o, b("sela"), [[-1, 1024]], A.is_ge, 0.0, 15 - 1024 * h, 16), "sela", "xpd%d" % h)
+    writer["xpd"] = writer["xpd1"]
+    act(b("bo16"), b("bo"), F.Copy, "bo", "bo16", scale=16.0)
+
+    def scalar_constants():
+        act(b("nbo"), b("bo"), F.Copy, "bo", "nbo", scale=-1.0)
+        act(b("idg"), b("id1"), F.Copy, "id1", "idg", scale=0.125)
+        act(b("idn"), b("id1"), F.Copy, "id1", "idn", scale=-1.0)
+        act(b("id32"), b("id1"), F.Copy, "id1", "id32")
+        act(b("id256"), b("id1"), F.Copy, "id1", "id256", scale=256.0)
+        act(b("idu"), b("id1"), F.Copy, "id1", "idu", scale=0.0625)
+        act(b("idn16"), b("id1"), F.Copy, "id1", "idn16", scale=-16.0)
+        act(b("c15b"), b("c15f"), F.Copy, "c15f", "c15b")
+        act(b("c15x16"), b("c15f"), F.Copy, "c15f", "c15x16", scale=16.0)
+        act(b("bo32"), b("bo"), F.Copy, "bo", "bo32")
+        act(b("one32"), b("one"), F.Copy, "one", "one32")
+        act(b("lims8", 0, 8), b("bo", 0, 128, 16), F.Identity, "bo limf", "lims8", scale=b("limf", 0, 1))
+        act(b("rs32"), b("rs32"), F.Sign, "rs32", "rs32")
+        for k in range(4): act(T.sg0[:, 256 * k:256 * k + 256], b("rs16"), F.Identity, "rs16", "sg0%d" % k, bias=-8192.0, scale=8193.0)
+        act(b("wput"), b("zt2"), F.Copy, "zt2", "wput", scale=-1.0)
+        act(b("dkc"), b("mq"), F.Identity, "mq", "dkc", bias=-6336.0, scale=8192.0)
+
+    def scalar_constants2():
+        act(b("bc2", 0, 8), b("bo", 0, 128, 16), F.Copy, "bo", "bc2a", scale=-1024.0)
+        act(b("bc2", 8, 16), b("bo", 0, 128, 16), F.Copy, "bo", "bc2b", scale=-1024.0)
+        act(b("id64"), b("id1"), F.Copy, "id1", "id64", scale=64.0)
+        act(b("idn64"), b("id1"), F.Copy, "id1", "idn64", scale=-64.0)
+        act(b("idm"), b("id1"), F.Copy, "id1", "idm", scale=-3712.0)
+        act(b("idn32"), b("id1"), F.Copy, "id1", "idn32", scale=-1.0)
+        act(b("pow2"), b("powf"), F.Copy, "powf", "pow2")
+
+    def vector_constants():
+        ts(b("limf", 0, 1), T.limi[:, 0:1], -0.0625, None, A.mult, None, "limi", "limf")
+        ts(b("bco31", 0, 8), b("bcoi", 0, 8), 32.0, 31.0, A.mult, A.add, "bcoi", "bco31")
+        ts(b("si2"), b("si0"), 15, None, A.bitwise_and, None, "si0", "si2")
+        ts(b("mqi"), b("d0i"), 15, None, A.bitwise_and, None, "d0i", "mqi")
+        tt(b("si3"), b("si2"), b("si1"), A.add, "si2 si1", "si3")
+        ts(b("mq"), b("mqi"), 0.0, None, A.is_equal, None, "mqi", "mq")
+        tc(b("selo"), b("si3"), "si3", "selo")
+
+    XR = "Xl0 Xl1 Xl2 X "
+
+    def gather(q, x, off, h, first, n, sc=None):
+        a = 64 * h + first
+        o = T[x][:, 16 * a:16 * (a + n)]; i = T.X[:, 0:XW].indirect(b(off, a, a + n)); W = "%s_%d%s" % (x, h, q)
+        if q == "v":
+            if sc is None: tc(o, i, XR + off, W)
+            else: ts(o, i, sc[0], sc[1], A.mult, A.add, XR + off, W)
+        elif sc is None: act(o, i, F.Copy, XR + off, W)
+        else: act(o, i, F.Identity, XR + off, W, bias=sc[1], scale=sc[0])
+
+    X1K = "x1_0v x1_0s x1_1v x1_1s "
+
+    def sums_T(h):
+        o = T.B2[:, 256 + 64 * h:320 + 64 * h]
+        for m in range(16):
+            mm(o, b("id1"), T.x1[:, 1024 * h + m:1024 * h + 1024:16], m == 0, False, X1K + "id1", "B2")
+        mm(o, b("bo"), b("emp", 64 * h, 64 * h + 64), False, True, "bo emp", "B2")
+
+    def sixteenth_T():
+        act(b("tsb"), T.B2[:, 256:384], F.Identity, "B2", "tsb", bias=-7.5)
+        act(b("tr"), b("tsb"), F.Identity, "tsb", "tr", bias=BIGM, scale=0.0625)
+        act(b("tf"), b("tr"), F.Identity, "tr", "tf", bias=-BIGM)
+
+    def drug_s():
+        mm(T.B5[:, 0:128], b("ohs"), b("id1"), True, True, "ohs id1", "B5")
+        tt(b("yds"), T.B5[:, 0:128], b("d16"), A.mult, "B5 d16", "yds")
+
+    def tables():
+        mm(T.B5[:, 128:136], b("yds"), b("bo", 0, 128, 16), True, True, "yds bo", "B5")
+        act(b("dsc", 0, 8), T.B5[:, 128:136], F.Copy, "B5", "dsc")
+        for w in range(8):
+            k = "B%d" % (6 + w // 4); c = w % 4 * 128
+            mm(T[k][:, c:c + 128], b("sel", 128 * w, 128 * w + 128), b("yds"), True, True, "sel yds", k)
+
+    def equal(w):
+        k = "B%d" % (6 + w // 4); c = w % 4 * 128
+        ts(b("ebuf", 128 * w, 128 * w + 128), T[k][:, c:c + 128], b("dsc", w, w + 1), None, A.is_equal, None, k + " dsc", "eb%d" % w)
+
+    def step5_list():
+        for w in range(8):
+            mm(T.B5[:, 136 + w:137 + w], b("ebuf", 128 * w, 128 * w + 128), b("wt", w, w + 1), True, True, "eb%d wt" % w, "B5")
+        ts(b("u1", 0, 8), b("dsc", 0, 8), b("pcol", 0, 1), None, A.subtract, None, "dsc pcol", "u1")
+        ts(b("fst", 0, 8), T.B5[:, 136:144], b("thr", 0, 1), None, A.is_lt, None, "B5 thr", "fst")
+        tt(b("fs", 0, 8), b("fst", 0, 8), b("stc", 0, 8), A.mult, "fst stc", "fs")
+        tt(b("u2", 0, 8), b("u1", 0, 8), b("fs", 0, 8), A.mult, "u1 fs", "u2")
+        ts(b("u3", 0, 8), b("u2", 0, 8), b("pcol", 0, 1), None, A.add, None, "u2 pcol", "u3")
+        tt(b("zl"), b("u3", 0, 8).indirect(b("bco", 0, 8)), b("mq"), A.mult, "u3 bco mq", "zl")
+        mm(T.B5[:, 144:152], b("zl"), b("bo32", 0, 128, 16), True, True, "zl bo32", "B5")
+        ts(b("dls", 0, 8), T.B5[:, 144:152], 1856.0, None, A.add, None, "B5", "dls")
+
+    def step5_write(x):
+        R = XR if x == "X" else "X2 "
+        tt(b("xni"), T[x][:, 0:XW].indirect(b("dls", 0, 8)), b("tf"), A.add, R + "dls tf", "xni")
+        ts(b("xnh"), b("xni"), 1, None, A.arith_shift_right, None, "xni", "xnh")
+        tc(T[x][:, 0:XW].indirect(b("dls", 0, 8)), b("xnh"), R + "dls xnh", x)
+
+    def send(t1, src, dst, kind):
+        need("g", [src], [])
+        tr = []
+        for h, s in ((0, S1), (1, S2)):
+            to = T.cores[(rank + s) % NR]
+            e = topo.engines(core, to); e = e[len(e) // 2 * h:len(e) // 2 * (h + 1)][:4]
+            rid, pid, _ = topo.addr(to)
+            tr.append(RemoteDMATransfer(dst_ids=[DstId(rid=rid, pnc=pid)], dma_engine_mask=sum(1 << i for i in e),
+                                        remote_sem=T.sem["arr%s%d" % (kind, t1)], src=T[src][:, 64 * h:64 * h + 64], dst=T[dst][:, 64 * h:64 * h + 64]))
+        g.remote_dma_fused(tr, local_sem=T.sem["loc%s%d" % (kind, t1)])
+        total["loc%s%d" % (kind, t1)] = 8; total["arr%s%d" % (kind, t1)] = 8
+        writer[dst] = ("arr%s%d" % (kind, t1), 8, "remote"); readers[dst] = []
+
+    for t in range(VI):
+        last = t == VI - 1
+        LD, LA, LW = "LD%d" % t, "LA%d" % t, "LW%d" % t
+        ACS = "acs" if t else "v0"
+        if last: dma("y", T.X2[:, :], T.X[:, :], XR, "X2")
+        mm(T.B0[:, 0:256], row("one"), row("c15r"), True, False, "one c15r", "B0")
+        if t == 0:
+            closure(14, 15)
+            tc(b("LD0"), b("drg"), "drg", "LD0")
+            ts(b("emp"), b("LD0"), 3712.0, None, A.is_equal, None, "LD0", "emp")
+            ts(b("d16"), b("LD0"), -1856.0, None, A.add, None, "LD0", "d16")
+            closure(11, 13)
+            vector_constants()
+            for h in range(2): gather("s", "x1", LD, h, 0, 64)
+            scalar_constants()
+        else:
+            gather("v", "x1", LD, 0, 0, VS1); gather("s", "x1", LD, 0, VS1, 64 - VS1)
+            ts(b("emp"), b(LD), 3712.0, None, A.is_equal, None, LD, "emp")
+            ts(b("d16"), b(LD), -1856.0, None, A.add, None, LD, "d16")
+            gather("v", "x1", LD, 1, 0, VS1); gather("s", "x1", LD, 1, VS1, 64 - VS1)
+            tc(b("cnti", 0, 1), b("cnt", 0, 1), "cnt", "cnti")
+            ts(b("cntj", 0, 1), b("cnti", 0, 1), 255, None, A.bitwise_and, None, "cnti", "cntj")
+            ts(b("cb", 0, 1), b("cntj", 0, 1), -1.0, 0.5, A.mult, A.add, "cntj", "cb")
+        mm(T.B7[:, 0:128], b("bo"), b("emp"), True, True, "bo emp", "B7")
+        mm(T.B2[:, 0:8], b("one32"), b("lims8", 0, 8), True, False, "one32 lims8", "B2")
+        mm(T.B2[:, 0:8], b("emp"), b("bo16", 0, 128, 16), False, False, "emp bo16", "B2")
+        mm(T.B1[:, 0:128], b("id1"), b("d16"), True, False, "id1 d16", "B1")
+        for m in range(16):
+            mm(T.B0[:, m:256:16], T.x1[:, m:2048:16], b("bo16", 0, 128, 8), False, m == 15, X1K + "bo16", "B0")
+        if t:
+            mm(T.B5[:, 384:512], b(LA), b("id32"), True, True, LA + " id32", "B5")
+        act(b("r1"), T.B7[:, 0:128], F.Relu, "B7", "r1", bias=8192.0, scale=-8192.0)
+        act(b("r2"), T.B7[:, 0:128], F.Relu, "B7", "r2", bias=-15 * 8192.0, scale=8192.0)
+        mm(T.B2[:, 0:8], b("r1"), b("bo", 0, 128, 16), False, False, "r1 bo", "B2")
+        mm(T.B2[:, 0:8], b("r2"), b("nbo", 0, 128, 16), False, False, "r2 nbo", "B2")
+        for m in range(16):
+            mm(T.B2[:, 0:8], T.x1[:, m:2048:16], b("bo", 0, 128, 16), False, m == 15, X1K + "bo", "B2")
+        if t:
+            act(b("acs"), T.B5[:, 384:512], F.Copy, "B5", "acs")
+        act(b("sgn", 0, 8), T.B2[:, 0:8], F.Sign, "B2 cb", "sgn", bias=b("cb", 0, 1))
+        act(b("st"), b("sgn", 0, 8).indirect(b("bco", 0, 8)), F.Relu, "sgn bco", "st")
+        if t == 0: closure(0, 10)
+        scan(b("key1"), b("rs32"), T.B0[:, 0:256], 0.0, A.mult, A.max, "rs32 B0", "key1")
+        tt(b("oh"), T.B0[:, 0:256], b("key1"), A.is_equal, "B0 key1", "oh")
+        act(b("ohs"), b("oh").indirect(b("selo", 0, 8)), F.Copy, "oh selo", "ohs")
+        scan(b("hor"), b("rs2"), b("oh"), 0.0, A.mult, A.add, "rs2 oh", "hor")
+        tt(b("zi"), b("hor").indirect(b("bco31", 0, 8)), b(ACS), A.mult, "hor bco31 " + ACS, "zi")
+        ts(b("gi"), b("zi"), 32768, None, A.bitwise_and, None, "zi", "gi")
+        tt(b("gs"), b("gi"), b("st"), A.mult, "gi st", "gs")
+        mm(T.B1[:, 0:128], b("gs"), b("idg"), False, True, "gs idg", "B1")
+        drug_s()
+        ts(b("offp"), T.B1[:, 0:128], 1856.0, 3712.0, A.add, A.min, "B1", "offp")
+        tables()
+        sc = (16.0, -2048.0)
+        gather("v", "x2", "offp", 0, 0, VS2, sc); gather("s", "x2", "offp", 0, VS2, 64 - VS2, sc)
+        gather("v", "x2", "offp", 1, 0, VS2, sc)
+        act(b("sg1"), T.B1[:, 0:128], F.Sign, "B1", "sg1", bias=-1855.5)
+        act(b("emq"), b("sg1"), F.Relu, "sg1", "emq")
+        gather("s", "x2", "offp", 1, VS2, 64 - VS2, sc)
+        act(b("stc", 0, 8), b("sgn", 0, 8), F.Relu, "sgn", "stc")
+        act(b("wt", 0, 8), b("stc", 0, 8), F.Identity, "stc wcol", "wt", scale=b("wcol", 0, 1))
+        mm(T.B4[:, 0:128], row("one"), row("c15x16"), True, False, "one c15x16", "B4")
+        for h in range(2):
+            for m in range(16):
+                mm(T.B3[:, 128 + 64 * h:192 + 64 * h], b("idu"), T.x2[:, 1024 * h + m:1024 * h + 1024:16], m == 0, False,
+                   "idu x2_%dv x2_%ds" % (h, h), "B3")
+            mm(T.B3[:, 128 + 64 * h:192 + 64 * h], b("bo"), b("emq", 64 * h, 64 * h + 64), False, True, "bo emq", "B3")
+        for h in range(2):
+            scan(T.sig[:, 1024 * h:1024 * h + 1024], T.sg0[:, 0:1024], T.x2[:, 1024 * h:1024 * h + 1024], 0.0, A.add, A.max,
+                 "sg00 sg01 sg02 sg03 x2_%dv x2_%ds" % (h, h), "sig%d" % h)
+        ts(b("r16"), T.sig[:, 15:2048:16], 0.0625, 1536 - 15 / 32, A.mult, A.add, "sig0 sig1", "r16")
+        act(b("usb"), T.B3[:, 128:256], F.Identity, "B3", "usb", bias=2168.5)
+        mm(T.B4[:, 0:128], b("usb"), b("id256"), False, False, "usb id256", "B4")
+        mm(T.B4[:, 0:128], T.sig[:, 15:2048:16], b("id1"), False, False, "sig0 sig1 id1", "B4")
+        mm(T.B5[:, 256:384], b("bo"), b("emq"), True, True, "bo emq", "B5")
+        mm(T.B4[:, 0:128], b("r16"), b("idn16"), False, True, "r16 idn16", "B4")
+        act(b("rq"), T.B5[:, 256:384], F.Relu, "B5", "rq", bias=-15.0)
+        act(b("ur"), b("usb"), F.Identity, "usb", "ur", bias=BIGM - 8, scale=0.0625)
+        act(b("wa"), b("ur"), F.Identity, "ur", "wa", bias=BIGM + 255, scale=-1.0)
+        mm(T.B5[:, 256:384], b("emq"), b("id1"), True, False, "emq id1", "B5")
+        mm(T.B5[:, 256:384], b("emq"), b("wput"), False, False, "emq wput", "B5")
+        mm(T.B5[:, 256:384], b("rq"), b("nbo"), False, True, "rq nbo", "B5")
+        act(b("put2", 0, 128), T.B5[:, 256:384], F.Relu, "B5", "put2a")
+        act(b("put2", 128, 256), b("put2", 0, 128), F.Copy, "put2a", "put2b")
+        sums_T(1)
+        for w in range(4): equal(w)
+        scan(b("skm"), b("rs16", 0, 128), T.B4[:, 0:128], 0.0, A.mult, A.max, "rs16 B4", "skm")
+        tc(b("kki", 0, 8), b("skm", 15, 128, 16), "skm", "kki")
+        ts(b("kk4", 0, 8), b("kki", 0, 8), 15, None, A.bitwise_and, None, "kki", "kk4")
+        tt(b("ohk"), b("kk4", 0, 8).indirect(b("bco", 0, 8)), b("c15b"), A.is_equal, "kk4 bco c15b", "ohk")
+        mm(T.B4[:, 128:256], b("ohk"), b("id1"), True, True, "ohk id1", "B4")
+        mm(T.B2[:, 128:256], b("id1"), b("dkc"), True, False, "id1 dkc", "B2")
+        ts(b("d16p"), b("offp"), -1856.0, None, A.add, None, "offp", "d16p")
+        tt(b("yd"), T.B4[:, 128:256], b("d16"), A.mult, "B4 d16", "yd")
+        mm(T.B0[:, 256:512], row("one"), row("cj1"), True, False, "one cj1", "B0")
+        mm(T.B2[:, 128:256], b("bo"), b("yd"), False, True, "bo yd", "B2")
+        mm(T.B0[:, 256:512], row("one"), row("cj2"), False, False, "one cj2", "B0")
+        mm(T.B1[:, 128:256], b("id1"), b("d16p"), True, False, "id1 d16p", "B1")
+        scan(b("dks"), b("rs16", 0, 128), T.B2[:, 128:256], 0.0, A.mult, A.max, "rs16 B2", "dks")
+        ts(b("dkl", 0, 8), b("dks", 15, 128, 16), 3711.0, None, A.min, None, "dks", "dkl")
+        tc(b("cand"), T.RM[:, :].indirect(b("dkl", 0, 8)), "RM dkl", "cand")
+        mm(T.B5[:, 384:512], b("wa"), b("idn"), True, True, "wa idn", "B5")
+        act(b("wc"), T.B5[:, 384:512], F.Copy, "B5", "wc")
+        sums_T(0)
+        act(b("ohkb"), T.B4[:, 128:256], F.Copy, "B4", "ohkb")
+        if t == 0:
+            scalar_constants2()
+            mm(T.B5[:, 256:384], b("v0"), b("id32"), True, True, "v0 id32", "B5")
+            act(b("LA0"), T.B5[:, 256:384], F.Copy, "B5", "LA0")
+        lo = 128 if last else 0
+        SD, SA, SW = "SD%d" % (t + 1), "SA%d" % (t + 1), "SW%d" % (t + 1)
+
+        def base(c):
+            q, a, n = CH[c]
+            o = T.B4[:, 256:512] if CB[c] == "B4" else T[CB[c]][:, 0:16 * n]
+            mm(o, b("wc"), T.xpd[:, 16 * a:16 * (a + n)], True, False, "wc xpd", CB[c])
+
+        def effects(c):
+            q, a, n = CH[c]
+            o = T.dif[:, 16 * a:16 * (a + n)]; i = T.X[:, 0:XW].indirect(b("cand", a, a + n))
+            if q == "v": tc(o, i, XR + "cand", "dif%d" % c)
+            else: act(o, i, F.Copy, XR + "cand", "dif%d" % c)
+
+        base(0); base(1)
+        for c in range(len(CH)):
+            if CH[c][0] == "s": effects(c)
+        for c in range(len(CH)):
+            q, a, n = CH[c]
+            if q == "v": effects(c)
+            if 1 < c < 4: base(c)
+            o = T.B4[:, 256:512] if CB[c] == "B4" else T[CB[c]][:, 0:16 * n]
+            mm(o, b("id1"), T.dif[:, 16 * a:16 * (a + n)], False, True, "id1 dif%d" % c, CB[c])
+            act(T.adf[:, 16 * a:16 * (a + n)], o, F.Abs, CB[c], "adf%d" % c)
+            if c == 1: base(4)
+            if c == 3:
+                ts(b("hi16"), b("cand"), 1 / 64, 1536 - 31.5 / 64, A.mult, A.add, "cand", "hi16")
+                ts(b("c16"), b("cand"), -1856.0, None, A.add, None, "cand", "c16")
+                mm(T.B0[:, 256:384], b("hi16"), b("id1"), False, False, "hi16 id1", "B0")
+                mm(T.B0[:, 384:512], b("c16"), b("id1"), False, False, "c16 id1", "B0")
+                mm(T.B0[:, 384:512], b("hi16"), b("idn64"), False, False, "hi16 idn64", "B0")
+                mm(T.B1[:, 128:256], b("put2", 0, 128), b("idm"), False, False, "put2a idm", "B1")
+            if c == 2 and last:
+                sixteenth_T()
+                for w in range(4, 8): equal(w)
+                step5_list()
+                step5_write("X2")
+                dma("y", T.yx[:, :], T.X2[:, 0:D], "X2", "yx")
+        for j in range(16):
+            mm(T.B0[:, 256 + j:512:16], T.adf[:, j:2048:16], b("bc2"), False, j == 15, "adf0 adf1 adf2 adf3 adf4 bc2a bc2b", "B0")
+        mm(T.B5[:, 256:384], b("put2", 0, 128), b("id1"), True, True, "put2a id1", "B5")
+        for h in range(2): act(b("putb", 128 * h, 128 * h + 128), T.B5[:, 256:384], F.Copy, "B5", "putb%d" % h)
+        if not last:
+            sixteenth_T()
+            mm(T.B5[:, 152:160], b("one"), b("stc", 0, 8), True, True, "one stc", "B5")
+            act(b("cjunk", 0, 8), T.B5[:, 152:160], F.Copy, "B5", "cjunk cnt", acc=b("cnt", 0, 1))
+        if not last:
+            for w in range(4, 8): equal(w)
+            tt(b("ya"), b("ohkb"), b(LA), A.mult, "ohkb " + LA, "ya")
+        mm(T.B4[:, 384:512], b("bom"), b("ohkb"), True, False, "bom ohkb", "B4")
+        mm(T.B4[:, 384:512], b("idn"), b(LW), False, True, "idn " + LW, "B4")
+        scan(b("scm"), b("rs16"), T.B0[:, 256:512], 0.0, A.mult, A.max, "rs16 B0", "scm")
+        tc(b("mi"), b("scm", 15, 256, 16), "scm", "mi")
+        ts(b("p63"), b("mi"), 63, None, A.bitwise_and, None, "mi", "p63")
+        tt(b("zz"), b("p63").indirect(b("bco", 0, 16)), b("put2"), A.mult, "p63 bco put2a put2b", "zz")
+        mm(T.B1[:, 128:256], b("zz", 0, 128), b("id64"), False, False, "zz id64", "B1")
+        mm(T.B1[:, 128:256], b("zz", 128, 256), b("id1"), False, True, "zz id1", "B1")
+        if last:
+            ts(b("yps"), T.B1[:, 128:256], 1856.0, None, A.add, None, "B1", "yps")
+            dma("y", T.yp[:, :], b("yps"), "yps", "yp")
+            ts(b("fil"), b("yps"), 3712.0, None, A.is_lt, None, "yps", "fil")
+        else:
+            ts(b(SD), T.B1[:, 128:256], 1856.0, None, A.add, None, "B1", SD)
+            send(t + 1, SD, "LD%d" % (t + 1), "D")
+            mm(T.B4[:, 256:384], b("bo32"), b("ya"), True, False, "bo32 ya", "B4")
+            mm(T.B4[:, 256:384], row("pow2"), row("one"), False, False, "pow2 one", "B4")
+            mm(T.B4[:, 256:384], b("idn32"), b(LA), False, True, "idn32 " + LA, "B4")
+            step5_list()
+        tt(b("aw1", lo, 256), T.B4[:, 256 + lo:512], b("putb", lo, 256), A.mult, "B4 putb0 putb1", "aw1")
+        if not last:
+            mm(T.B3[:, 0:128], b("id32"), b("aw1", 0, 128), True, False, "id32 aw1", "B3")
+            mm(T.B3[:, 0:128], b("id32"), b(LA), False, True, "id32 " + LA, "B3")
+            act(b(SA), T.B3[:, 0:128], F.Copy, "B3", SA)
+            send(t + 1, SA, "LA%d" % (t + 1), "A")
+        mm(T.B6[:, 0:128], b("id32"), b("aw1", 128, 256), True, False, "id32 aw1", "B6")
+        mm(T.B6[:, 0:128], b("id1"), b(LW), False, True, "id1 " + LW, "B6")
+        if last:
+            tt(b("yqs"), T.B6[:, 0:128], b("fil"), A.mult, "B6 fil", "yqs")
+            dma("s", T.yq[:, :], b("yqs"), "yqs", "yq")
+        else:
+            act(b(SW), T.B6[:, 0:128], F.Copy, "B6", SW)
+            send(t + 1, SW, "LW%d" % (t + 1), "W")
+            step5_write("X")
+    for sem in SEMAPHORES:
+        if total.get(sem, 0) > known["g"].get(sem, 0): g.wait_ge(T.sem[sem], total[sem])

@@ -5,7 +5,7 @@ import comms_topo
 D, VI, S1, S2, NR = 3712, 4, 3, 5, 8
 XW = 3856
 BIGM = 12582912.0
-VS2, VS1 = 36, 32
+VS2, VS1 = 40, 30
 
 SCRATCH = {}
 PLACE = {}
@@ -32,14 +32,14 @@ for _k in range(VI):
     _own("uint16", 128, "LD%d" % _k); _own("float32", 128, "LA%d" % _k); _own("bfloat16", 128, "LW%d" % _k)
     if _k: _own("uint16", 128, "SD%d" % _k); _own("float32", 128, "SA%d" % _k); _own("bfloat16", 128, "SW%d" % _k)
 _own("int32", 128, "drg whyi"); _own("float32", 128, "yps yqs"); _own("int32", 8, "limi")
-_small("int32", 128, "d0i mqi zi gi xni xnh bcoi"); _small("int32", 16, "mi p63 kki kk4 cnti cntj si0 si1 si2 si3")
+_small("int32", 128, "d0i mqi zi gi xni xnh bcoi skm"); _small("int32", 256, "scm"); _small("int32", 16, "p63 kk4 cnti cntj si0 si1 si2 si3")
 _small("uint16", 128, "bco offp cand"); _small("uint16", 16, "bco31 selo dkl dls")
 _small("bfloat16", 128, "one zt1 zt2 bo bo16 nbo bom id1 idn id64 idg idm idu idn16 idn64 wput mq dkc c15b c15x16 pow2 emp r1 r2 "
-       "ohs gs st sg1 emq rq ohk ohkb tf wa wc e0")
-_small("bfloat16", 256, "c15r rs32 rs16 rs2 cj1 cj2 put2 putb zz oh"); _small("bfloat16", 1024, "onesel sela sel ebuf")
-_small("bfloat16", 16, "bc2 stc wt"); _small("float16", 128, "d16 d16p yd r16 hi16 c16 yds")
-_small("float32", 128, "d0 t0 id32 idn32 id256 bo32 one32 powf pwr half zero acs usb ur tsb tr skm dks ya zl fil v0 vt vm wc1 neq c15f nrs mf")
-_small("float32", 256, "key1 hor scm aw1"); _small("float32", 16, "limf lims8 sgn cb cnt cjunk dsc fst fs u1 u2 u3 wcol thr pcol smv")
+       "ohs gs st sg1 emq rq ohk ohkb tf wa wc e0 awb")
+_small("bfloat16", 256, "c15r rs32 rs16 rs2 cj1 cj2 put2 zz oh"); _small("bfloat16", 128, "putb"); _small("bfloat16", 1024, "onesel sela sel ebuf")
+_small("bfloat16", 16, "bc2 stc wt"); _small("float16", 128, "d16 d16p yd r16 hi16 c16 yds"); _small("float16", 16, "pc16")
+_small("float32", 128, "d0 t0 id32 idn32 id256 bo32 one32 powf pwr half zero acs usb ur tsb tr dks ya zl fil v0 vt vm wc1 neq c15f nrs mf")
+_small("float32", 256, "key1 hor"); _small("float32", 128, "aw1"); _small("float32", 16, "limf lims8 sgn cb cnt cjunk dsc fst fs u1 u2 u3 wcol thr pcol smv")
 for _k in range(8): SCRATCH["B%d" % _k] = ("psum", [128, 512], "float32")
 
 SEMAPHORES = ["qv", "qs", "qp", "qg"] + ["arr%s%d" % (a, t) for a in "DAW" for t in range(1, VI)] \
@@ -171,6 +171,7 @@ def rank_program(g, core, T, topo):
     sel("bo", "zt1", [[16, 8], [0, 16]], 15, -1)
     iota("c15r", [[0, 16], [-1, 16]], 15, 0)
     iota("rs32", [[0, 8], [1, 32]], 0, 0)
+    iota("pcol", [[0, 16]], 1864, 1)
     iota("si0", [[0, 16]], 0, 1)
     iota("si1", [[32, 16]], 16, 0)
     iota("d0i", [[-1, 128]], 0, 1)
@@ -181,7 +182,6 @@ def rank_program(g, core, T, topo):
     sel("bom", "zt1", [[16, 8], [0, 16]], 15, -1)
     iota("cj2", [[0, 16], [-64, 16]], 0, 0)
     iota("cj1", [[0, 256]], 4325376, 0)
-    iota("pcol", [[0, 16]], 1864, 1)
     op("g", lambda: g.iota(b("onesel"), [[0, 1024]], 1, 0, allow_small_or_imprecise_dtypes=True), "", "onesel")
     sel("sela", "onesel", [[-16, 8], [0, 128]], 0, 1)
     sel("sel", "sela", [[16, 8], [0, 128]], 15, -1)
@@ -221,6 +221,7 @@ def rank_program(g, core, T, topo):
 
     def vector_constants():
         ts(b("limf", 0, 1), T.limi[:, 0:1], -0.0625, None, A.mult, None, "limi", "limf")
+        ts(b("pc16", 0, 8), b("bo", 0, 128, 16), b("pcol", 0, 1), None, A.mult, None, "bo pcol", "pc16")
         ts(b("bco31", 0, 8), b("bcoi", 0, 8), 32.0, 31.0, A.mult, A.add, "bcoi", "bco31")
         ts(b("si2"), b("si0"), 15, None, A.bitwise_and, None, "si0", "si2")
         ts(b("mqi"), b("d0i"), 15, None, A.bitwise_and, None, "d0i", "mqi")
@@ -267,16 +268,20 @@ def rank_program(g, core, T, topo):
         k = "B%d" % (6 + w // 4); c = w % 4 * 128
         ts(b("ebuf", 128 * w, 128 * w + 128), T[k][:, c:c + 128], b("dsc", w, w + 1), None, A.is_equal, None, k + " dsc", "eb%d" % w)
 
-    def step5_list():
+    def list_first():
         for w in range(8):
             mm(T.B5[:, 136 + w:137 + w], b("ebuf", 128 * w, 128 * w + 128), b("wt", w, w + 1), True, True, "eb%d wt" % w, "B5")
         ts(b("u1", 0, 8), b("dsc", 0, 8), b("pcol", 0, 1), None, A.subtract, None, "dsc pcol", "u1")
+        tt(b("u3", 0, 8), b("u1", 0, 8), b("stc", 0, 8), A.mult, "u1 stc", "u3")
+
+    def list_next():
         ts(b("fst", 0, 8), T.B5[:, 136:144], b("thr", 0, 1), None, A.is_lt, None, "B5 thr", "fst")
-        tt(b("fs", 0, 8), b("fst", 0, 8), b("stc", 0, 8), A.mult, "fst stc", "fs")
-        tt(b("u2", 0, 8), b("u1", 0, 8), b("fs", 0, 8), A.mult, "u1 fs", "u2")
-        ts(b("u3", 0, 8), b("u2", 0, 8), b("pcol", 0, 1), None, A.add, None, "u2 pcol", "u3")
-        tt(b("zl"), b("u3", 0, 8).indirect(b("bco", 0, 8)), b("mq"), A.mult, "u3 bco mq", "zl")
-        mm(T.B5[:, 144:152], b("zl"), b("bo32", 0, 128, 16), True, True, "zl bo32", "B5")
+        tt(b("u2", 0, 8), b("u3", 0, 8), b("fst", 0, 8), A.mult, "u3 fst", "u2")
+        tt(b("zl"), b("u2", 0, 8).indirect(b("bco", 0, 8)), b("mq"), A.mult, "u2 bco mq", "zl")
+        mm(T.B5[:, 144:152], b("mq"), b("pc16", 0, 8), True, False, "mq pc16", "B5")
+        mm(T.B5[:, 144:152], b("zl"), b("bo32", 0, 128, 16), False, True, "zl bo32", "B5")
+
+    def list_last():
         ts(b("dls", 0, 8), T.B5[:, 144:152], 1856.0, None, A.add, None, "B5", "dls")
 
     def step5_write(x):
@@ -339,7 +344,9 @@ def rank_program(g, core, T, topo):
             act(b("acs"), T.B5[:, 384:512], F.Copy, "B5", "acs")
         act(b("sgn", 0, 8), T.B2[:, 0:8], F.Sign, "B2 cb", "sgn", bias=b("cb", 0, 1))
         act(b("st"), b("sgn", 0, 8).indirect(b("bco", 0, 8)), F.Relu, "sgn bco", "st")
-        if t == 0: closure(0, 10)
+        if t == 0:
+            scalar_constants2()
+            closure(0, 10)
         scan(b("key1"), b("rs32"), T.B0[:, 0:256], 0.0, A.mult, A.max, "rs32 B0", "key1")
         tt(b("oh"), T.B0[:, 0:256], b("key1"), A.is_equal, "B0 key1", "oh")
         act(b("ohs"), b("oh").indirect(b("selo", 0, 8)), F.Copy, "oh selo", "ohs")
@@ -359,6 +366,8 @@ def rank_program(g, core, T, topo):
         gather("s", "x2", "offp", 1, VS2, 64 - VS2, sc)
         act(b("stc", 0, 8), b("sgn", 0, 8), F.Relu, "sgn", "stc")
         act(b("wt", 0, 8), b("stc", 0, 8), F.Identity, "stc wcol", "wt", scale=b("wcol", 0, 1))
+        mm(T.B0[:, 256:512], row("one"), row("cj1"), True, False, "one cj1", "B0")
+        mm(T.B0[:, 256:512], row("one"), row("cj2"), False, False, "one cj2", "B0")
         mm(T.B4[:, 0:128], row("one"), row("c15x16"), True, False, "one c15x16", "B4")
         for h in range(2):
             for m in range(16):
@@ -377,37 +386,29 @@ def rank_program(g, core, T, topo):
         act(b("rq"), T.B5[:, 256:384], F.Relu, "B5", "rq", bias=-15.0)
         act(b("ur"), b("usb"), F.Identity, "usb", "ur", bias=BIGM - 8, scale=0.0625)
         act(b("wa"), b("ur"), F.Identity, "ur", "wa", bias=BIGM + 255, scale=-1.0)
-        mm(T.B5[:, 256:384], b("emq"), b("id1"), True, False, "emq id1", "B5")
-        mm(T.B5[:, 256:384], b("emq"), b("wput"), False, False, "emq wput", "B5")
-        mm(T.B5[:, 256:384], b("rq"), b("nbo"), False, True, "rq nbo", "B5")
-        act(b("put2", 0, 128), T.B5[:, 256:384], F.Relu, "B5", "put2a")
-        act(b("put2", 128, 256), b("put2", 0, 128), F.Copy, "put2a", "put2b")
         sums_T(1)
         for w in range(4): equal(w)
         scan(b("skm"), b("rs16", 0, 128), T.B4[:, 0:128], 0.0, A.mult, A.max, "rs16 B4", "skm")
-        tc(b("kki", 0, 8), b("skm", 15, 128, 16), "skm", "kki")
-        ts(b("kk4", 0, 8), b("kki", 0, 8), 15, None, A.bitwise_and, None, "kki", "kk4")
+        ts(b("kk4", 0, 8), b("skm", 15, 128, 16), 15, None, A.bitwise_and, None, "skm", "kk4")
         tt(b("ohk"), b("kk4", 0, 8).indirect(b("bco", 0, 8)), b("c15b"), A.is_equal, "kk4 bco c15b", "ohk")
         mm(T.B4[:, 128:256], b("ohk"), b("id1"), True, True, "ohk id1", "B4")
         mm(T.B2[:, 128:256], b("id1"), b("dkc"), True, False, "id1 dkc", "B2")
         ts(b("d16p"), b("offp"), -1856.0, None, A.add, None, "offp", "d16p")
         tt(b("yd"), T.B4[:, 128:256], b("d16"), A.mult, "B4 d16", "yd")
-        mm(T.B0[:, 256:512], row("one"), row("cj1"), True, False, "one cj1", "B0")
         mm(T.B2[:, 128:256], b("bo"), b("yd"), False, True, "bo yd", "B2")
-        mm(T.B0[:, 256:512], row("one"), row("cj2"), False, False, "one cj2", "B0")
+        mm(T.B1[:, 256:384], b("wa"), b("idn"), True, True, "wa idn", "B1")
+        act(b("wc"), T.B1[:, 256:384], F.Copy, "B1", "wc")
+        mm(T.B5[:, 256:384], b("emq"), b("id1"), True, False, "emq id1", "B5")
+        mm(T.B5[:, 256:384], b("emq"), b("wput"), False, False, "emq wput", "B5")
+        mm(T.B5[:, 256:384], b("rq"), b("nbo"), False, True, "rq nbo", "B5")
+        act(b("put2", 0, 128), T.B5[:, 256:384], F.Relu, "B5", "put2a")
+        act(b("put2", 128, 256), b("put2", 0, 128), F.Copy, "put2a", "put2b")
         mm(T.B1[:, 128:256], b("id1"), b("d16p"), True, False, "id1 d16p", "B1")
         scan(b("dks"), b("rs16", 0, 128), T.B2[:, 128:256], 0.0, A.mult, A.max, "rs16 B2", "dks")
         ts(b("dkl", 0, 8), b("dks", 15, 128, 16), 3711.0, None, A.min, None, "dks", "dkl")
         tc(b("cand"), T.RM[:, :].indirect(b("dkl", 0, 8)), "RM dkl", "cand")
-        mm(T.B5[:, 384:512], b("wa"), b("idn"), True, True, "wa idn", "B5")
-        act(b("wc"), T.B5[:, 384:512], F.Copy, "B5", "wc")
         sums_T(0)
         act(b("ohkb"), T.B4[:, 128:256], F.Copy, "B4", "ohkb")
-        if t == 0:
-            scalar_constants2()
-            mm(T.B5[:, 256:384], b("v0"), b("id32"), True, True, "v0 id32", "B5")
-            act(b("LA0"), T.B5[:, 256:384], F.Copy, "B5", "LA0")
-        lo = 128 if last else 0
         SD, SA, SW = "SD%d" % (t + 1), "SA%d" % (t + 1), "SW%d" % (t + 1)
 
         def base(c):
@@ -424,6 +425,8 @@ def rank_program(g, core, T, topo):
         base(0); base(1)
         for c in range(len(CH)):
             if CH[c][0] == "s": effects(c)
+        mm(T.B5[:, 128:256], b("put2", 0, 128), b("id1"), True, True, "put2a id1", "B5")
+        act(b("putb"), T.B5[:, 128:256], F.Copy, "B5", "putb")
         for c in range(len(CH)):
             q, a, n = CH[c]
             if q == "v": effects(c)
@@ -431,7 +434,17 @@ def rank_program(g, core, T, topo):
             o = T.B4[:, 256:512] if CB[c] == "B4" else T[CB[c]][:, 0:16 * n]
             mm(o, b("id1"), T.dif[:, 16 * a:16 * (a + n)], False, True, "id1 dif%d" % c, CB[c])
             act(T.adf[:, 16 * a:16 * (a + n)], o, F.Abs, CB[c], "adf%d" % c)
-            if c == 1: base(4)
+            if c == 1:
+                base(4)
+                mm(T.B5[:, 0:128], b("bom"), b("ohkb"), True, False, "bom ohkb", "B5")
+                mm(T.B5[:, 0:128], b("idn"), b(LW), False, True, "idn " + LW, "B5")
+            if c == 3:
+                tt(b("awb"), T.B5[:, 0:128], b("putb"), A.mult, "B5 putb", "awb")
+                mm(T.B5[:, 0:128], b("id1"), b("awb"), True, False, "id1 awb", "B5")
+                mm(T.B5[:, 0:128], b("id1"), b(LW), False, True, "id1 " + LW, "B5")
+                if not last:
+                    act(b(SW), T.B5[:, 0:128], F.Copy, "B5", SW)
+                    send(t + 1, SW, "LW%d" % (t + 1), "W")
             if c == 3:
                 ts(b("hi16"), b("cand"), 1 / 64, 1536 - 31.5 / 64, A.mult, A.add, "cand", "hi16")
                 ts(b("c16"), b("cand"), -1856.0, None, A.add, None, "cand", "c16")
@@ -442,13 +455,14 @@ def rank_program(g, core, T, topo):
             if c == 2 and last:
                 sixteenth_T()
                 for w in range(4, 8): equal(w)
-                step5_list()
+                list_first(); list_next(); list_last()
                 step5_write("X2")
                 dma("y", T.yx[:, :], T.X2[:, 0:D], "X2", "yx")
         for j in range(16):
             mm(T.B0[:, 256 + j:512:16], T.adf[:, j:2048:16], b("bc2"), False, j == 15, "adf0 adf1 adf2 adf3 adf4 bc2a bc2b", "B0")
-        mm(T.B5[:, 256:384], b("put2", 0, 128), b("id1"), True, True, "put2a id1", "B5")
-        for h in range(2): act(b("putb", 128 * h, 128 * h + 128), T.B5[:, 256:384], F.Copy, "B5", "putb%d" % h)
+        if t == 0:
+            mm(T.B5[:, 256:384], b("v0"), b("id32"), True, True, "v0 id32", "B5")
+            act(b("LA0"), T.B5[:, 256:384], F.Copy, "B5", "LA0")
         if not last:
             sixteenth_T()
             mm(T.B5[:, 152:160], b("one"), b("stc", 0, 8), True, True, "one stc", "B5")
@@ -456,11 +470,9 @@ def rank_program(g, core, T, topo):
         if not last:
             for w in range(4, 8): equal(w)
             tt(b("ya"), b("ohkb"), b(LA), A.mult, "ohkb " + LA, "ya")
-        mm(T.B4[:, 384:512], b("bom"), b("ohkb"), True, False, "bom ohkb", "B4")
-        mm(T.B4[:, 384:512], b("idn"), b(LW), False, True, "idn " + LW, "B4")
+            list_first()
         scan(b("scm"), b("rs16"), T.B0[:, 256:512], 0.0, A.mult, A.max, "rs16 B0", "scm")
-        tc(b("mi"), b("scm", 15, 256, 16), "scm", "mi")
-        ts(b("p63"), b("mi"), 63, None, A.bitwise_and, None, "mi", "p63")
+        ts(b("p63"), b("scm", 15, 256, 16), 63, None, A.bitwise_and, None, "scm", "p63")
         tt(b("zz"), b("p63").indirect(b("bco", 0, 16)), b("put2"), A.mult, "p63 bco put2a put2b", "zz")
         mm(T.B1[:, 128:256], b("zz", 0, 128), b("id64"), False, False, "zz id64", "B1")
         mm(T.B1[:, 128:256], b("zz", 128, 256), b("id1"), False, True, "zz id1", "B1")
@@ -468,27 +480,21 @@ def rank_program(g, core, T, topo):
             ts(b("yps"), T.B1[:, 128:256], 1856.0, None, A.add, None, "B1", "yps")
             dma("y", T.yp[:, :], b("yps"), "yps", "yp")
             ts(b("fil"), b("yps"), 3712.0, None, A.is_lt, None, "yps", "fil")
+            tt(b("yqs"), T.B5[:, 0:128], b("fil"), A.mult, "B5 fil", "yqs")
+            dma("s", T.yq[:, :], b("yqs"), "yqs", "yq")
         else:
             ts(b(SD), T.B1[:, 128:256], 1856.0, None, A.add, None, "B1", SD)
             send(t + 1, SD, "LD%d" % (t + 1), "D")
             mm(T.B4[:, 256:384], b("bo32"), b("ya"), True, False, "bo32 ya", "B4")
             mm(T.B4[:, 256:384], row("pow2"), row("one"), False, False, "pow2 one", "B4")
             mm(T.B4[:, 256:384], b("idn32"), b(LA), False, True, "idn32 " + LA, "B4")
-            step5_list()
-        tt(b("aw1", lo, 256), T.B4[:, 256 + lo:512], b("putb", lo, 256), A.mult, "B4 putb0 putb1", "aw1")
-        if not last:
-            mm(T.B3[:, 0:128], b("id32"), b("aw1", 0, 128), True, False, "id32 aw1", "B3")
-            mm(T.B3[:, 0:128], b("id32"), b(LA), False, True, "id32 " + LA, "B3")
+            list_next()
+            tt(b("aw1"), T.B4[:, 256:384], b("putb"), A.mult, "B4 putb", "aw1")
+            list_last()
+            mm(T.B3[:, 0:128], b("id32"), b(LA), True, False, "id32 " + LA, "B3")
+            mm(T.B3[:, 0:128], b("id32"), b("aw1"), False, True, "id32 aw1", "B3")
             act(b(SA), T.B3[:, 0:128], F.Copy, "B3", SA)
             send(t + 1, SA, "LA%d" % (t + 1), "A")
-        mm(T.B6[:, 0:128], b("id32"), b("aw1", 128, 256), True, False, "id32 aw1", "B6")
-        mm(T.B6[:, 0:128], b("id1"), b(LW), False, True, "id1 " + LW, "B6")
-        if last:
-            tt(b("yqs"), T.B6[:, 0:128], b("fil"), A.mult, "B6 fil", "yqs")
-            dma("s", T.yq[:, :], b("yqs"), "yqs", "yq")
-        else:
-            act(b(SW), T.B6[:, 0:128], F.Copy, "B6", SW)
-            send(t + 1, SW, "LW%d" % (t + 1), "W")
             step5_write("X")
     for sem in SEMAPHORES:
         if total.get(sem, 0) > known["g"].get(sem, 0): g.wait_ge(T.sem[sem], total[sem])

from concourse.bass import DstId, RemoteDMATransfer
from concourse.mybir import dt, AluOpType, AxisListType, ActivationFunctionType
import comms_topo

D, VI, S1, S2, NR = 3712, 4, 3, 5, 8
XW = 3856
BIGM = 12582912.0
VS2, VS1 = 40, 30

SCRATCH = {}
PLACE = {}
_used = {}


def _own(dtype, cols, names):
    for n in names.split():
        SCRATCH[n] = ("sbuf", [128, cols], dtype); PLACE[n] = (n, 0, cols)


def _small(dtype, cols, names):
    for n in names.split():
        a = _used.get(dtype, 0)
        PLACE[n] = ("pool_" + dtype, a, cols); _used[dtype] = a + (cols + 15) // 16 * 16
        SCRATCH["pool_" + dtype] = ("sbuf", [128, _used[dtype]], dtype)


_own("bfloat16", XW, "X X2"); _own("int32", D, "RM")
CH = (("v", 0, 32), ("s", 32, 24), ("v", 56, 32), ("v", 88, 24), ("v", 112, 16))
CB = ("B3", "B6", "B3", "B6", "B4")
_own("bfloat16", 2048, "x1 x2 xpd dif adf sg0"); _own("float16", 2048, "sig")
for _k in range(VI):
    _own("uint16", 128, "LD%d" % _k); _own("float32", 128, "LA%d" % _k); _own("bfloat16", 128, "LW%d" % _k)
    if _k: _own("uint16", 128, "SD%d" % _k); _own("float32", 128, "SA%d" % _k); _own("bfloat16", 128, "SW%d" % _k)
_own("int32", 128, "drg whyi"); _own("float32", 128, "yps yqs"); _own("int32", 8, "limi")
_small("int32", 128, "d0i mqi zi gi xni xnh bcoi skm"); _small("int32", 256, "scm"); _small("int32", 16, "p63 kk4 cnti cntj si0 si1 si2 si3")
_small("uint16", 128, "bco offp cand"); _small("uint16", 16, "bco31 selo dkl dls")
_small("bfloat16", 128, "one zt1 zt2 bo bo16 nbo bom id1 idn id64 idg idm idu idn16 idn64 wput mq dkc c15b c15x16 pow2 emp r1 r2 "
       "ohs gs st sg1 emq rq ohk ohkb tf wa wc e0 awb")
_small("bfloat16", 256, "c15r rs32 rs16 rs2 cj1 cj2 put2 zz oh"); _small("bfloat16", 128, "putb"); _small("bfloat16", 1024, "onesel sela sel ebuf")
_small("bfloat16", 16, "bc2 stc wt"); _small("float16", 128, "d16 d16p yd r16 hi16 c16 yds"); _small("float16", 16, "pc16")
_small("float32", 128, "d0 t0 id32 idn32 id256 bo32 one32 powf pwr half zero acs usb ur tsb tr dks ya zl fil v0 vt vm wc1 neq c15f nrs mf")
_small("float32", 256, "key1 hor"); _small("float32", 128, "aw1"); _small("float32", 16, "limf lims8 sgn cb cnt cjunk dsc fst fs u1 u2 u3 wcol thr pcol smv")
for _k in range(8): SCRATCH["B%d" % _k] = ("psum", [128, 512], "float32")

SEMAPHORES = ["qv", "qs", "qp", "qg"] + ["arr%s%d" % (a, t) for a in "DAW" for t in range(1, VI)] \
    + ["loc%s%d" % (a, t) for a in "DAW" for t in range(1, VI)] + ["dm%d" % i for i in range(11)]


def rank_program(g, core, T, topo):
    rank = T.rank_of(core)
    if rank is None:
        return
    A = AluOpType; F = ActivationFunctionType
    V, S, P = g.vector, g.scalar, g.tensor
    q_of = {"v": V, "s": S, "p": P, "g": g, "y": g.sync}
    cnt = {"v": 0, "s": 0, "p": 0, "g": 0}
    known = {q: {} for q in q_of}
    writer = {}; readers = {}; snap = {}; total = {}

    def b(name, lo=0, hi=None, step=None):
        n, o, w = PLACE[name]
        hi = w if hi is None else hi
        return T[n][:, o + lo:o + hi] if step is None else T[n][:, o + lo:o + hi:step]

    def row(name, lo=0, hi=None):
        n, o, w = PLACE[name]
        return T[n][0:1, o + lo:o + (w if hi is None else hi)]

    def need(q, R, W):
        deps = []
        for k in R:
            if k in writer: deps.append(writer[k])
            if k[0] == "B": deps += [r for r in readers.get(k, []) if r[2] != q]
        for k in W:
            if k in writer: deps.append(writer[k])
            deps += readers.get(k, [])
        for sem, val, dq in deps:
            if q == "p" and dq == "p": continue
            if known[q].get(sem, 0) >= val: continue
            q_of[q].wait_ge(T.sem[sem], val)
            known[q][sem] = val
            for s2, v2 in snap.get((sem, val), {}).items():
                if known[q].get(s2, 0) < v2: known[q][s2] = v2

    def done(q, R, W, sem, val, who):
        snap[(sem, val)] = dict(known[q]); total[sem] = val
        for k in R: readers.setdefault(k, []).append((sem, val, who))
        for k in W:
            writer[k] = (sem, val, who); readers[k] = []

    def op(q, f, R, W):
        R = R.split(); W = W.split()
        need(q, R, W)
        cnt[q] += 1
        f().then_inc(T.sem["q" + q], 1)
        done(q, R, W, "q" + q, cnt[q], q)

    ndma = [0]

    def dma(q, out, in_, R, W):
        R = R.split(); W = W.split()
        need(q, R, W)
        sem = "dm%d" % ndma[0]; ndma[0] += 1
        q_of[q].dma_start(out, in_).then_inc(T.sem[sem], 16)
        done(q, R, W, sem, 16, "dma")

    def ts(out, in0, s1, s2, o0, o1, R, W):
        if o1 is None: op("v", lambda: V.tensor_scalar(out, in0, s1, None, o0), R, W)
        else: op("v", lambda: V.tensor_scalar(out, in0, s1, s2, o0, o1), R, W)

    def tt(out, in0, in1, o, R, W): op("v", lambda: V.tensor_tensor(out, in0, in1, o), R, W)

    def tc(out, in_, R, W): op("v", lambda: V.tensor_copy(out, in_), R, W)

    def scan(out, d0, d1, init, o0, o1, R, W): op("v", lambda: V.tensor_tensor_scan(out, d0, d1, init, o0, o1), R, W)

    def act(out, in_, fn, R, W, bias=0.0, scale=1.0, acc=None):
        if acc is None: op("s", lambda: S.activation(out, in_, fn, bias=bias, scale=scale), R, W)
        else: op("s", lambda: S.activation(out, in_, fn, bias=bias, scale=scale, accum_out=acc), R, W)

    def mm(out, l, r, start, stop, R, W): op("p", lambda: P.matmul(out, l, r, start, stop), R, W)

    def fill(name, c): op("v", lambda: V.memset(b(name), c), "", name)

    def iota(name, pattern, base, cm):
        if "int32" in PLACE[name][0]: op("g", lambda: g.iota(b(name), pattern, base, cm), "", name)
        else: op("g", lambda: g.iota(b(name), pattern, base, cm, allow_small_or_imprecise_dtypes=True), "", name)

    def sel(out, in_, pattern, base, cm): op("g", lambda: g.affine_select(b(out), b(in_), pattern, A.is_ge, 0.0, base, cm), in_, out)

    dma("s", b("whyi"), T.why[:, :], "", "whyi")
    dma("y", b("drg"), T.drugs[:, :], "", "drg")
    dma("s", T.X[:, 0:1856], T.eff[:, 0:1856], "", "Xl0")
    dma("y", T.X[:, 1856:D], T.eff[:, 1856:D], "", "Xl1")
    dma("y", T.limi[:, 0:1], T.lim[:, :], "", "limi")
    dma("y", T.RM[:, :], T.rem[:, :], "", "RM")

    op("v", lambda: V.memset(T.X[:, D:XW], -1.0), "", "Xl2")
    fill("one", 1.0); fill("half", 0.5); fill("zero", 0.0); fill("cb", 0.5)
    scan(b("pwr"), b("half"), b("zero"), 2.0 ** 64, A.mult, A.add, "half zero", "pwr")
    iota("rs16", [[0, 16], [1, 16]], 0, 0)
    iota("d0", [[-1, 128]], 0, 1)
    iota("bcoi", [[1, 128]], 0, 0)
    iota("mf", [[0, 8], [1, 16]], 0, 0)
    ts(b("rs16"), b("rs16"), 0.0, None, A.is_gt, None, "rs16", "rs16")
    ts(b("rs2"), b("rs16"), 2.0, None, A.mult, None, "rs16", "rs2")
    ts(b("nrs"), b("rs16", 0, 128), -1.0, 1.0, A.mult, A.add, "rs16", "nrs")
    scan(b("powf"), b("rs2", 0, 128), b("nrs"), 0.0, A.mult, A.add, "rs2 nrs", "powf")
    ts(b("id1"), b("d0"), 0.0, None, A.is_equal, None, "d0", "id1")
    tc(b("bco"), b("bcoi"), "bcoi", "bco")
    tt(b("t0"), b("pwr"), b("id1"), A.mult, "pwr id1", "t0")
    op("v", lambda: V.tensor_reduce(b("wcol", 0, 1), b("t0"), AxisListType.X, A.add), "t0", "wcol")
    ts(b("thr", 0, 1), b("wcol", 0, 1), 2.5, None, A.mult, None, "wcol", "thr")
    tc(b("LW0"), b("whyi"), "whyi", "LW0")
    mm(T.B5[:, 384:512], b("LW0"), b("id1"), True, True, "LW0 id1", "B5")
    tt(b("neq"), T.B5[:, 384:512], b("mf"), A.not_equal, "B5 mf", "neq")
    ts(b("wc1"), T.B5[:, 384:512], 1.0, 65536.0, A.add, A.mult, "B5", "wc1")
    tt(b("vt"), b("wc1"), b("neq"), A.mult, "wc1 neq", "vt")
    tt(T.B6[:, 0:128], b("vt"), b("powf"), A.add, "vt powf", "B6")

    def closure(lo, hi):
        for c in range(hi, lo - 1, -1):
            K = 65536.0 * (c + 1)
            ts(b("smv", 0, 8), T.B6[:, c:128:16], -K, None, A.add, None, "B6", "smv")
            ts(b("vm"), T.B6[:, 0:128], K, None, A.is_ge, None, "B6", "vm")
            tt(b("vt"), b("smv").indirect(b("bco", 0, 8)), b("vm"), A.mult, "smv bco vm", "vt")
            if c: tt(T.B6[:, 0:128], T.B6[:, 0:128], b("vt"), A.add, "B6 vt", "B6")
            else: tt(b("v0"), T.B6[:, 0:128], b("vt"), A.add, "B6 vt", "v0")

    sel("zt1", "one", [[-16, 8], [0, 16]], 0, 1)
    sel("bo", "zt1", [[16, 8], [0, 16]], 15, -1)
    iota("c15r", [[0, 16], [-1, 16]], 15, 0)
    iota("rs32", [[0, 8], [1, 32]], 0, 0)
    iota("pcol", [[0, 16]], 1864, 1)
    iota("si0", [[0, 16]], 0, 1)
    iota("si1", [[32, 16]], 16, 0)
    iota("d0i", [[-1, 128]], 0, 1)
    iota("c15f", [[0, 8], [-1, 16]], 15, 0)
    op("g", lambda: g.affine_select(b("zt2"), b("bo"), [[1, 128]], A.is_ge, 0.0, -1, -1), "bo", "zt2")
    iota("e0", [[-16, 8], [0, 16]], 0, 1)
    sel("zt1", "e0", [[-16, 8], [0, 16]], 0, 1)
    sel("bom", "zt1", [[16, 8], [0, 16]], 15, -1)
    iota("cj2", [[0, 16], [-64, 16]], 0, 0)
    iota("cj1", [[0, 256]], 4325376, 0)
    op("g", lambda: g.iota(b("onesel"), [[0, 1024]], 1, 0, allow_small_or_imprecise_dtypes=True), "", "onesel")
    sel("sela", "onesel", [[-16, 8], [0, 128]], 0, 1)
    sel("sel", "sela", [[16, 8], [0, 128]], 15, -1)
    for h in range(2):
        o = T.xpd[:, 1024 * h:1024 * h + 1024]
        op("g", lambda: g.affine_select(b("sela"), b("onesel"), [[1, 1024]], A.is_ge, 0.0, 1024 * h, -16), "onesel", "sela")
        op("g", lambda: g.affine_select(o, b("sela"), [[-1, 1024]], A.is_ge, 0.0, 15 - 1024 * h, 16), "sela", "xpd%d" % h)
    writer["xpd"] = writer["xpd1"]
    act(b("bo16"), b("bo"), F.Copy, "bo", "bo16", scale=16.0)

    def scalar_constants():
        act(b("nbo"), b("bo"), F.Copy, "bo", "nbo", scale=-1.0)
        act(b("idg"), b("id1"), F.Copy, "id1", "idg", scale=0.125)
        act(b("idn"), b("id1"), F.Copy, "id1", "idn", scale=-1.0)
        act(b("id32"), b("id1"), F.Copy, "id1", "id32")
        act(b("id256"), b("id1"), F.Copy, "id1", "id256", scale=256.0)
        act(b("idu"), b("id1"), F.Copy, "id1", "idu", scale=0.0625)
        act(b("idn16"), b("id1"), F.Copy, "id1", "idn16", scale=-16.0)
        act(b("c15b"), b("c15f"), F.Copy, "c15f", "c15b")
        act(b("c15x16"), b("c15f"), F.Copy, "c15f", "c15x16", scale=16.0)
        act(b("bo32"), b("bo"), F.Copy, "bo", "bo32")
        act(b("one32"), b("one"), F.Copy, "one", "one32")
        act(b("lims8", 0, 8), b("bo", 0, 128, 16), F.Identity, "bo limf", "lims8", scale=b("limf", 0, 1))
        act(b("rs32"), b("rs32"), F.Sign, "rs32", "rs32")
        for k in range(4): act(T.sg0[:, 256 * k:256 * k + 256], b("rs16"), F.Identity, "rs16", "sg0%d" % k, bias=-8192.0, scale=8193.0)
        act(b("wput"), b("zt2"), F.Copy, "zt2", "wput", scale=-1.0)
        act(b("dkc"), b("mq"), F.Identity, "mq", "dkc", bias=-6336.0, scale=8192.0)

    def scalar_constants2():
        act(b("bc2", 0, 8), b("bo", 0, 128, 16), F.Copy, "bo", "bc2a", scale=-1024.0)
        act(b("bc2", 8, 16), b("bo", 0, 128, 16), F.Copy, "bo", "bc2b", scale=-1024.0)
        act(b("id64"), b("id1"), F.Copy, "id1", "id64", scale=64.0)
        act(b("idn64"), b("id1"), F.Copy, "id1", "idn64", scale=-64.0)
        act(b("idm"), b("id1"), F.Copy, "id1", "idm", scale=-3712.0)
        act(b("idn32"), b("id1"), F.Copy, "id1", "idn32", scale=-1.0)
        act(b("pow2"), b("powf"), F.Copy, "powf", "pow2")

    def vector_constants():
        ts(b("limf", 0, 1), T.limi[:, 0:1], -0.0625, None, A.mult, None, "limi", "limf")
        ts(b("pc16", 0, 8), b("bo", 0, 128, 16), b("pcol", 0, 1), None, A.mult, None, "bo pcol", "pc16")
        ts(b("bco31", 0, 8), b("bcoi", 0, 8), 32.0, 31.0, A.mult, A.add, "bcoi", "bco31")
        ts(b("si2"), b("si0"), 15, None, A.bitwise_and, None, "si0", "si2")
        ts(b("mqi"), b("d0i"), 15, None, A.bitwise_and, None, "d0i", "mqi")
        tt(b("si3"), b("si2"), b("si1"), A.add, "si2 si1", "si3")
        ts(b("mq"), b("mqi"), 0.0, None, A.is_equal, None, "mqi", "mq")
        tc(b("selo"), b("si3"), "si3", "selo")

    XR = "Xl0 Xl1 Xl2 X "

    def gather(q, x, off, h, first, n, sc=None):
        a = 64 * h + first
        o = T[x][:, 16 * a:16 * (a + n)]; i = T.X[:, 0:XW].indirect(b(off, a, a + n)); W = "%s_%d%s" % (x, h, q)
        if q == "v":
            if sc is None: tc(o, i, XR + off, W)
            else: ts(o, i, sc[0], sc[1], A.mult, A.add, XR + off, W)
        elif sc is None: act(o, i, F.Copy, XR + off, W)
        else: act(o, i, F.Identity, XR + off, W, bias=sc[1], scale=sc[0])

    X1K = "x1_0v x1_0s x1_1v x1_1s "

    def sums_T(h):
        o = T.B2[:, 256 + 64 * h:320 + 64 * h]
        for m in range(16):
            mm(o, b("id1"), T.x1[:, 1024 * h + m:1024 * h + 1024:16], m == 0, False, X1K + "id1", "B2")
        mm(o, b("bo"), b("emp", 64 * h, 64 * h + 64), False, True, "bo emp", "B2")

    def sixteenth_T():
        act(b("tsb"), T.B2[:, 256:384], F.Identity, "B2", "tsb", bias=-7.5)
        act(b("tr"), b("tsb"), F.Identity, "tsb", "tr", bias=BIGM, scale=0.0625)
        act(b("tf"), b("tr"), F.Identity, "tr", "tf", bias=-BIGM)

    def drug_s():
        mm(T.B5[:, 0:128], b("ohs"), b("id1"), True, True, "ohs id1", "B5")
        tt(b("yds"), T.B5[:, 0:128], b("d16"), A.mult, "B5 d16", "yds")

    def tables():
        mm(T.B5[:, 128:136], b("yds"), b("bo", 0, 128, 16), True, True, "yds bo", "B5")
        act(b("dsc", 0, 8), T.B5[:, 128:136], F.Copy, "B5", "dsc")
        for w in range(8):
            k = "B%d" % (6 + w // 4); c = w % 4 * 128
            mm(T[k][:, c:c + 128], b("sel", 128 * w, 128 * w + 128), b("yds"), True, True, "sel yds", k)

    def equal(w):
        k = "B%d" % (6 + w // 4); c = w % 4 * 128
        ts(b("ebuf", 128 * w, 128 * w + 128), T[k][:, c:c + 128], b("dsc", w, w + 1), None, A.is_equal, None, k + " dsc", "eb%d" % w)

    def list_first():
        for w in range(8):
            mm(T.B5[:, 136 + w:137 + w], b("ebuf", 128 * w, 128 * w + 128), b("wt", w, w + 1), True, True, "eb%d wt" % w, "B5")
        ts(b("u1", 0, 8), b("dsc", 0, 8), b("pcol", 0, 1), None, A.subtract, None, "dsc pcol", "u1")
        tt(b("u3", 0, 8), b("u1", 0, 8), b("stc", 0, 8), A.mult, "u1 stc", "u3")

    def list_next():
        ts(b("fst", 0, 8), T.B5[:, 136:144], b("thr", 0, 1), None, A.is_lt, None, "B5 thr", "fst")
        tt(b("u2", 0, 8), b("u3", 0, 8), b("fst", 0, 8), A.mult, "u3 fst", "u2")
        tt(b("zl"), b("u2", 0, 8).indirect(b("bco", 0, 8)), b("mq"), A.mult, "u2 bco mq", "zl")
        mm(T.B5[:, 144:152], b("mq"), b("pc16", 0, 8), True, False, "mq pc16", "B5")
        mm(T.B5[:, 144:152], b("zl"), b("bo32", 0, 128, 16), False, True, "zl bo32", "B5")

    def list_last():
        ts(b("dls", 0, 8), T.B5[:, 144:152], 1856.0, None, A.add, None, "B5", "dls")

    def step5_write(x):
        R = XR if x == "X" else "X2 "
        tt(b("xni"), T[x][:, 0:XW].indirect(b("dls", 0, 8)), b("tf"), A.add, R + "dls tf", "xni")
        ts(b("xnh"), b("xni"), 1, None, A.arith_shift_right, None, "xni", "xnh")
        tc(T[x][:, 0:XW].indirect(b("dls", 0, 8)), b("xnh"), R + "dls xnh", x)

    def send(t1, src, dst, kind):
        need("g", [src], [])
        tr = []
        for h, s in ((0, S1), (1, S2)):
            to = T.cores[(rank + s) % NR]
            e = topo.engines(core, to); e = e[len(e) // 2 * h:len(e) // 2 * (h + 1)][:4]
            rid, pid, _ = topo.addr(to)
            tr.append(RemoteDMATransfer(dst_ids=[DstId(rid=rid, pnc=pid)], dma_engine_mask=sum(1 << i for i in e),
                                        remote_sem=T.sem["arr%s%d" % (kind, t1)], src=T[src][:, 64 * h:64 * h + 64], dst=T[dst][:, 64 * h:64 * h + 64]))
        g.remote_dma_fused(tr, local_sem=T.sem["loc%s%d" % (kind, t1)])
        total["loc%s%d" % (kind, t1)] = 8; total["arr%s%d" % (kind, t1)] = 8
        writer[dst] = ("arr%s%d" % (kind, t1), 8, "remote"); readers[dst] = []

    for t in range(VI):
        last = t == VI - 1
        LD, LA, LW = "LD%d" % t, "LA%d" % t, "LW%d" % t
        ACS = "acs" if t else "v0"
        if last: dma("y", T.X2[:, :], T.X[:, :], XR, "X2")
        mm(T.B0[:, 0:256], row("one"), row("c15r"), True, False, "one c15r", "B0")
        if t == 0:
            closure(14, 15)
            tc(b("LD0"), b("drg"), "drg", "LD0")
            ts(b("emp"), b("LD0"), 3712.0, None, A.is_equal, None, "LD0", "emp")
            ts(b("d16"), b("LD0"), -1856.0, None, A.add, None, "LD0", "d16")
            closure(11, 13)
            vector_constants()
            for h in range(2): gather("s", "x1", LD, h, 0, 64)
            scalar_constants()
        else:
            gather("v", "x1", LD, 0, 0, VS1); gather("s", "x1", LD, 0, VS1, 64 - VS1)
            ts(b("emp"), b(LD), 3712.0, None, A.is_equal, None, LD, "emp")
            ts(b("d16"), b(LD), -1856.0, None, A.add, None, LD, "d16")
            gather("v", "x1", LD, 1, 0, VS1); gather("s", "x1", LD, 1, VS1, 64 - VS1)
            tc(b("cnti", 0, 1), b("cnt", 0, 1), "cnt", "cnti")
            ts(b("cntj", 0, 1), b("cnti", 0, 1), 255, None, A.bitwise_and, None, "cnti", "cntj")
            ts(b("cb", 0, 1), b("cntj", 0, 1), -1.0, 0.5, A.mult, A.add, "cntj", "cb")
        mm(T.B7[:, 0:128], b("bo"), b("emp"), True, True, "bo emp", "B7")
        mm(T.B2[:, 0:8], b("one32"), b("lims8", 0, 8), True, False, "one32 lims8", "B2")
        mm(T.B2[:, 0:8], b("emp"), b("bo16", 0, 128, 16), False, False, "emp bo16", "B2")
        mm(T.B1[:, 0:128], b("id1"), b("d16"), True, False, "id1 d16", "B1")
        for m in range(16):
            mm(T.B0[:, m:256:16], T.x1[:, m:2048:16], b("bo16", 0, 128, 8), False, m == 15, X1K + "bo16", "B0")
        if t:
            mm(T.B5[:, 384:512], b(LA), b("id32"), True, True, LA + " id32", "B5")
        act(b("r1"), T.B7[:, 0:128], F.Relu, "B7", "r1", bias=8192.0, scale=-8192.0)
        act(b("r2"), T.B7[:, 0:128], F.Relu, "B7", "r2", bias=-15 * 8192.0, scale=8192.0)
        mm(T.B2[:, 0:8], b("r1"), b("bo", 0, 128, 16), False, False, "r1 bo", "B2")
        mm(T.B2[:, 0:8], b("r2"), b("nbo", 0, 128, 16), False, False, "r2 nbo", "B2")
        for m in range(16):
            mm(T.B2[:, 0:8], T.x1[:, m:2048:16], b("bo", 0, 128, 16), False, m == 15, X1K + "bo", "B2")
        if t:
            act(b("acs"), T.B5[:, 384:512], F.Copy, "B5", "acs")
        act(b("sgn", 0, 8), T.B2[:, 0:8], F.Sign, "B2 cb", "sgn", bias=b("cb", 0, 1))
        act(b("st"), b("sgn", 0, 8).indirect(b("bco", 0, 8)), F.Relu, "sgn bco", "st")
        if t == 0:
            scalar_constants2()
            closure(0, 10)
        scan(b("key1"), b("rs32"), T.B0[:, 0:256], 0.0, A.mult, A.max, "rs32 B0", "key1")
        tt(b("oh"), T.B0[:, 0:256], b("key1"), A.is_equal, "B0 key1", "oh")
        act(b("ohs"), b("oh").indirect(b("selo", 0, 8)), F.Copy, "oh selo", "ohs")
        scan(b("hor"), b("rs2"), b("oh"), 0.0, A.mult, A.add, "rs2 oh", "hor")
        tt(b("zi"), b("hor").indirect(b("bco31", 0, 8)), b(ACS), A.mult, "hor bco31 " + ACS, "zi")
        ts(b("gi"), b("zi"), 32768, None, A.bitwise_and, None, "zi", "gi")
        tt(b("gs"), b("gi"), b("st"), A.mult, "gi st", "gs")
        mm(T.B1[:, 0:128], b("gs"), b("idg"), False, True, "gs idg", "B1")
        drug_s()
        ts(b("offp"), T.B1[:, 0:128], 1856.0, 3712.0, A.add, A.min, "B1", "offp")
        tables()
        sc = (16.0, -2048.0)
        gather("v", "x2", "offp", 0, 0, VS2, sc); gather("s", "x2", "offp", 0, VS2, 64 - VS2, sc)
        gather("v", "x2", "offp", 1, 0, VS2, sc)
        act(b("sg1"), T.B1[:, 0:128], F.Sign, "B1", "sg1", bias=-1855.5)
        act(b("emq"), b("sg1"), F.Relu, "sg1", "emq")
        gather("s", "x2", "offp", 1, VS2, 64 - VS2, sc)
        act(b("stc", 0, 8), b("sgn", 0, 8), F.Relu, "sgn", "stc")
        act(b("wt", 0, 8), b("stc", 0, 8), F.Identity, "stc wcol", "wt", scale=b("wcol", 0, 1))
        mm(T.B0[:, 256:512], row("one"), row("cj1"), True, False, "one cj1", "B0")
        mm(T.B0[:, 256:512], row("one"), row("cj2"), False, False, "one cj2", "B0")
        mm(T.B4[:, 0:128], row("one"), row("c15x16"), True, False, "one c15x16", "B4")
        for h in range(2):
            for m in range(16):
                mm(T.B3[:, 128 + 64 * h:192 + 64 * h], b("idu"), T.x2[:, 1024 * h + m:1024 * h + 1024:16], m == 0, False,
                   "idu x2_%dv x2_%ds" % (h, h), "B3")
            mm(T.B3[:, 128 + 64 * h:192 + 64 * h], b("bo"), b("emq", 64 * h, 64 * h + 64), False, True, "bo emq", "B3")
        for h in range(2):
            scan(T.sig[:, 1024 * h:1024 * h + 1024], T.sg0[:, 0:1024], T.x2[:, 1024 * h:1024 * h + 1024], 0.0, A.add, A.max,
                 "sg00 sg01 sg02 sg03 x2_%dv x2_%ds" % (h, h), "sig%d" % h)
        ts(b("r16"), T.sig[:, 15:2048:16], 0.0625, 1536 - 15 / 32, A.mult, A.add, "sig0 sig1", "r16")
        act(b("usb"), T.B3[:, 128:256], F.Identity, "B3", "usb", bias=2168.5)
        mm(T.B4[:, 0:128], b("usb"), b("id256"), False, False, "usb id256", "B4")
        mm(T.B4[:, 0:128], T.sig[:, 15:2048:16], b("id1"), False, False, "sig0 sig1 id1", "B4")
        mm(T.B5[:, 256:384], b("bo"), b("emq"), True, True, "bo emq", "B5")
        mm(T.B4[:, 0:128], b("r16"), b("idn16"), False, True, "r16 idn16", "B4")
        act(b("rq"), T.B5[:, 256:384], F.Relu, "B5", "rq", bias=-15.0)
        act(b("ur"), b("usb"), F.Identity, "usb", "ur", bias=BIGM - 8, scale=0.0625)
        act(b("wa"), b("ur"), F.Identity, "ur", "wa", bias=BIGM + 255, scale=-1.0)
        sums_T(1)
        for w in range(4): equal(w)
        scan(b("skm"), b("rs16", 0, 128), T.B4[:, 0:128], 0.0, A.mult, A.max, "rs16 B4", "skm")
        ts(b("kk4", 0, 8), b("skm", 15, 128, 16), 15, None, A.bitwise_and, None, "skm", "kk4")
        tt(b("ohk"), b("kk4", 0, 8).indirect(b("bco", 0, 8)), b("c15b"), A.is_equal, "kk4 bco c15b", "ohk")
        mm(T.B4[:, 128:256], b("ohk"), b("id1"), True, True, "ohk id1", "B4")
        mm(T.B2[:, 128:256], b("id1"), b("dkc"), True, False, "id1 dkc", "B2")
        ts(b("d16p"), b("offp"), -1856.0, None, A.add, None, "offp", "d16p")
        tt(b("yd"), T.B4[:, 128:256], b("d16"), A.mult, "B4 d16", "yd")
        mm(T.B2[:, 128:256], b("bo"), b("yd"), False, True, "bo yd", "B2")
        mm(T.B1[:, 256:384], b("wa"), b("idn"), True, True, "wa idn", "B1")
        act(b("wc"), T.B1[:, 256:384], F.Copy, "B1", "wc")
        mm(T.B5[:, 256:384], b("emq"), b("id1"), True, False, "emq id1", "B5")
        mm(T.B5[:, 256:384], b("emq"), b("wput"), False, False, "emq wput", "B5")
        mm(T.B5[:, 256:384], b("rq"), b("nbo"), False, True, "rq nbo", "B5")
        act(b("put2", 0, 128), T.B5[:, 256:384], F.Relu, "B5", "put2a")
        act(b("put2", 128, 256), b("put2", 0, 128), F.Copy, "put2a", "put2b")
        mm(T.B1[:, 128:256], b("id1"), b("d16p"), True, False, "id1 d16p", "B1")
        scan(b("dks"), b("rs16", 0, 128), T.B2[:, 128:256], 0.0, A.mult, A.max, "rs16 B2", "dks")
        ts(b("dkl", 0, 8), b("dks", 15, 128, 16), 3711.0, None, A.min, None, "dks", "dkl")
        tc(b("cand"), T.RM[:, :].indirect(b("dkl", 0, 8)), "RM dkl", "cand")
        sums_T(0)
        act(b("ohkb"), T.B4[:, 128:256], F.Copy, "B4", "ohkb")
        SD, SA, SW = "SD%d" % (t + 1), "SA%d" % (t + 1), "SW%d" % (t + 1)

        def base(c):
            q, a, n = CH[c]
            o = T.B4[:, 256:512] if CB[c] == "B4" else T[CB[c]][:, 0:16 * n]
            mm(o, b("wc"), T.xpd[:, 16 * a:16 * (a + n)], True, False, "wc xpd", CB[c])

        def effects(c):
            q, a, n = CH[c]
            o = T.dif[:, 16 * a:16 * (a + n)]; i = T.X[:, 0:XW].indirect(b("cand", a, a + n))
            if q == "v": tc(o, i, XR + "cand", "dif%d" % c)
            else: act(o, i, F.Copy, XR + "cand", "dif%d" % c)

        base(0); base(1)
        for c in range(len(CH)):
            if CH[c][0] == "s": effects(c)
        mm(T.B5[:, 128:256], b("put2", 0, 128), b("id1"), True, True, "put2a id1", "B5")
        act(b("putb"), T.B5[:, 128:256], F.Copy, "B5", "putb")
        for c in range(len(CH)):
            q, a, n = CH[c]
            if q == "v": effects(c)
            if 1 < c < 4: base(c)
            o = T.B4[:, 256:512] if CB[c] == "B4" else T[CB[c]][:, 0:16 * n]
            mm(o, b("id1"), T.dif[:, 16 * a:16 * (a + n)], False, True, "id1 dif%d" % c, CB[c])
            act(T.adf[:, 16 * a:16 * (a + n)], o, F.Abs, CB[c], "adf%d" % c)
            if c == 1:
                base(4)
                mm(T.B5[:, 0:128], b("bom"), b("ohkb"), True, False, "bom ohkb", "B5")
                mm(T.B5[:, 0:128], b("idn"), b(LW), False, True, "idn " + LW, "B5")
            if c == 3:
                tt(b("awb"), T.B5[:, 0:128], b("putb"), A.mult, "B5 putb", "awb")
                mm(T.B5[:, 0:128], b("id1"), b("awb"), True, False, "id1 awb", "B5")
                mm(T.B5[:, 0:128], b("id1"), b(LW), False, True, "id1 " + LW, "B5")
                if not last:
                    act(b(SW), T.B5[:, 0:128], F.Copy, "B5", SW)
                    send(t + 1, SW, "LW%d" % (t + 1), "W")
            if c == 3:
                ts(b("hi16"), b("cand"), 1 / 64, 1536 - 31.5 / 64, A.mult, A.add, "cand", "hi16")
                ts(b("c16"), b("cand"), -1856.0, None, A.add, None, "cand", "c16")
                mm(T.B0[:, 256:384], b("hi16"), b("id1"), False, False, "hi16 id1", "B0")
                mm(T.B0[:, 384:512], b("c16"), b("id1"), False, False, "c16 id1", "B0")
                mm(T.B0[:, 384:512], b("hi16"), b("idn64"), False, False, "hi16 idn64", "B0")
                mm(T.B1[:, 128:256], b("put2", 0, 128), b("idm"), False, False, "put2a idm", "B1")
            if c == 2 and last:
                sixteenth_T()
                for w in range(4, 8): equal(w)
                list_first(); list_next(); list_last()
                step5_write("X2")
                dma("y", T.yx[:, :], T.X2[:, 0:D], "X2", "yx")
        for j in range(16):
            mm(T.B0[:, 256 + j:512:16], T.adf[:, j:2048:16], b("bc2"), False, j == 15, "adf0 adf1 adf2 adf3 adf4 bc2a bc2b", "B0")
        if t == 0:
            mm(T.B5[:, 256:384], b("v0"), b("id32"), True, True, "v0 id32", "B5")
            act(b("LA0"), T.B5[:, 256:384], F.Copy, "B5", "LA0")
        if not last:
            sixteenth_T()
            mm(T.B5[:, 152:160], b("one"), b("stc", 0, 8), True, True, "one stc", "B5")
            act(b("cjunk", 0, 8), T.B5[:, 152:160], F.Copy, "B5", "cjunk cnt", acc=b("cnt", 0, 1))
        if not last:
            for w in range(4, 8): equal(w)
            tt(b("ya"), b("ohkb"), b(LA), A.mult, "ohkb " + LA, "ya")
            list_first()
        scan(b("scm"), b("rs16"), T.B0[:, 256:512], 0.0, A.mult, A.max, "rs16 B0", "scm")
        ts(b("p63"), b("scm", 15, 256, 16), 63, None, A.bitwise_and, None, "scm", "p63")
        tt(b("zz"), b("p63").indirect(b("bco", 0, 16)), b("put2"), A.mult, "p63 bco put2a put2b", "zz")
        mm(T.B1[:, 128:256], b("zz", 0, 128), b("id64"), False, False, "zz id64", "B1")
        mm(T.B1[:, 128:256], b("zz", 128, 256), b("id1"), False, True, "zz id1", "B1")
        if last:
            ts(b("yps"), T.B1[:, 128:256], 1856.0, None, A.add, None, "B1", "yps")
            dma("y", T.yp[:, :], b("yps"), "yps", "yp")
            ts(b("fil"), b("yps"), 3712.0, None, A.is_lt, None, "yps", "fil")
            tt(b("yqs"), T.B5[:, 0:128], b("fil"), A.mult, "B5 fil", "yqs")
            dma("s", T.yq[:, :], b("yqs"), "yqs", "yq")
        else:
            ts(b(SD), T.B1[:, 128:256], 1856.0, None, A.add, None, "B1", SD)
            send(t + 1, SD, "LD%d" % (t + 1), "D")
            mm(T.B4[:, 256:384], b("bo32"), b("ya"), True, False, "bo32 ya", "B4")
            mm(T.B4[:, 256:384], row("pow2"), row("one"), False, False, "pow2 one", "B4")
            mm(T.B4[:, 256:384], b("idn32"), b(LA), False, True, "idn32 " + LA, "B4")
            list_next()
            tt(b("aw1"), T.B4[:, 256:384], b("putb"), A.mult, "B4 putb", "aw1")
            list_last()
            mm(T.B3[:, 0:128], b("id32"), b(LA), True, False, "id32 " + LA, "B3")
            mm(T.B3[:, 0:128], b("id32"), b("aw1"), False, True, "id32 aw1", "B3")
            act(b(SA), T.B3[:, 0:128], F.Copy, "B3", SA)
            send(t + 1, SA, "LA%d" % (t + 1), "A")
            step5_write("X")
    for sem in SEMAPHORES:
        if total.get(sem, 0) > known["g"].get(sem, 0): g.wait_ge(T.sem[sem], total[sem])
